import numpy as np, ml_dtypes
CORES = [13,21,141,149]
N = 4
BF = ml_dtypes.bfloat16
def gentries(a):
    return np.ascontiguousarray(a.reshape(8, 16, -1).transpose(0, 2, 1)).reshape(8, -1)
def gtable(e):
    e = np.asarray(e); return np.ascontiguousarray(e.reshape(8, -1, 16).transpose(0, 2, 1)).reshape(128, -1).astype(np.int32)
W, TB, K, DE = 4096, 192, 3, 2
def parts(rng):
    b = rng.integers(0, 128, (N, 8, 1, W)) + rng.integers(0, 129, (N, 8, 16, W))
    return np.minimum(b, 255), rng.integers(0, W, (N, 8, TB, 16)), rng.integers(0, N, (8, TB))
def pack(b, h, first):
    return {"bk": np.ascontiguousarray(b.reshape(N, 128, W)).astype(np.float32).astype(BF), "hand": np.stack([gtable(a.reshape(8, -1)) for a in h]),
            "ld": np.ascontiguousarray(np.tile(first[None], (N, 1, 1))).astype(np.int32)}
def setup_inputs(rng):
    b, h, first = parts(rng)
    return pack(b, h, first)
def setup_inputs_suits(rng):
    b, h, first = parts(rng); q = rng.integers(0, 4, (1, 8, TB, 1)); s = np.arange(N)[:, None, None, None]
    m = rng.integers(0, 4, (1, 8, TB, 1)); m[0, :, :4, 0] = np.arange(4)
    one = np.arange(16) == rng.integers(0, 16, (N, 8, TB, 1))
    su = np.where(m == 0, q, np.where(m == 1, (q + s) & 3, np.where(m == 2, np.where(one, q, (q + 1 + (h >> 2) % 3) & 3), h & 3)))
    return pack(b, (h >> 2) * 4 + su, first)
def setup_inputs_ties(rng):
    b, h, first = parts(rng); base = rng.integers(1, 255, (1, 8, 16, 1)); rot = rng.integers(0, 16, (N, 8, 1, W))
    m = rng.choice(np.array([0, 7, 8, 9, 9, 10, 16]), (N, 8, 1, W)); less = rng.integers(0, 2, (N, 8, 1, W))
    v = base + np.where(((np.arange(16)[:, None] + rot) & 15) < m, 1, -less)
    return pack(np.where(rng.random((N, 8, 1, W)) < 0.5, base, v), h, first)
def setup_inputs_alike(rng):
    b, h, first = parts(rng)
    h[:, 0] = (W - 1) * rng.integers(0, 2, (N, TB, 16)); h[:, 1] = h[:1, 1]; h[:, 2] = h[:, 2, :, :1]; h[:, 3] = h[:, 3, :1]
    h[:, 4] = rng.integers(0, 32, (N, TB, 16)); h[:, 5] = W - 1 - rng.integers(0, 16, (N, TB, 16))
    first[6] = 0; first[7] = N - 1
    return pack(b, h, first)
def setup_inputs_lords(rng):
    b, h, first = parts(rng); s = np.arange(N)[:, None, None, None]
    b[:, 0:2] = 7; b[:, 1, int(rng.integers(0, 16))] += rng.integers(0, 2, (N, W))
    b[:, 2:4] = 20 * s + rng.integers(0, 10, (N, 2, 16, W)); b[:, 4] = 255 * rng.integers(0, 2, (N, 1, W))
    b[:, 5] = 255 * (rng.random((N, 16, W)) < rng.random((N, 1, W)))
    m = rng.permutation(TB)[:, None]
    h = np.where(m < TB // 4, h | 255, np.where(m < TB // 2, h | 240, h))
    first[:] = rng.integers(0, N)
    return pack(b, h, first)
def setup_inputs_spread(rng):
    b, h, first = parts(rng)
    b = np.minimum((rng.random((N, 8, 16, W)) * np.exp2(rng.integers(0, 9, (N, 8, 1, W)))).astype(np.int64), 255)
    h = np.minimum((W * rng.random((N, 8, TB, 16)) ** 3).astype(np.int64), W - 1)
    return pack(b, h, np.minimum(first, rng.integers(0, N, (8, TB))))
def check_inputs(d):
    bad = []
    b = np.asarray(d["bk"]).astype(np.float32)
    if not np.all((b >= 0) & (b <= 255) & (b == np.floor(b))): bad.append("numbers of bk")
    for k, hi in (("hand", W - 1), ("ld", N - 1)):
        if np.min(d[k]) < 0 or np.max(d[k]) > hi: bad.append("range of " + k)
    if np.any(d["ld"] != d["ld"][:1]): bad.append("ld alike on all ranks")
    return bad
def reference(bk, hand, ld):
    B = np.asarray(bk).astype(np.float32).astype(np.int16).reshape(N, 8, 16, W)
    c = np.stack([gentries(a) for a in hand]).astype(np.int64).reshape(N, 8, TB, 16)
    lead = np.array(ld[0], np.int64); T = np.zeros(TB, np.int64); won = np.zeros((N, 8, TB), np.int64)
    e = np.zeros((N, 8, TB, 16), np.int64); beat = np.zeros((N, 8, TB, 16), bool); live = np.ones((N, 8, TB, 16), bool)
    S = np.arange(N)[:, None, None]; g = np.arange(8)[:, None]; t = np.arange(TB)[None, :]; R = np.arange(16)
    for deal in range(DE):
        rows, cards, wins = [], [], []
        for k in range(K):
            lr = np.argmax(np.where(live, e, -1), axis=3)[lead, g, t]
            L = c[lead, g, t, lr]; y = B[lead, g, :, L].transpose(0, 2, 1)[..., None]
            isl = S == lead
            live = live & ~(isl[..., None] & (R == lr[..., None]))
            a = ((c * L[..., None] >> 5) + c + 13 * T[:, None]) & (W - 1)
            for s in range(N):
                d = np.take_along_axis(B[s], a[s].reshape(8, 1, -1), 2).reshape(8, 16, TB, 16) - y
                e[s] = np.add.reduce(np.abs(d), axis=1, dtype=np.int64)
                beat[s] = np.add.reduce(d > 0, axis=1, dtype=np.int64) >= 9
            legal = live & ((c & 3) == (L & 3)[..., None])
            legal = np.where(np.any(legal, axis=3, keepdims=True), legal, live)
            good = legal & beat; has = np.any(good, axis=3) & ~isl
            row = np.where(has, np.argmin(np.where(good, e, 2 ** 20), axis=3), np.argmax(np.where(legal, e, -1), axis=3))
            row = np.where(isl, lr, row)[..., None]
            card = np.take_along_axis(c, row, 3)[..., 0]; score = np.where(has, np.take_along_axis(e, row, 3)[..., 0], -1)
            win = np.where(np.any(has, axis=0), np.argmax(score, axis=0), lead)
            live = live & (R != row)
            won = won + (S == win)
            T = np.add.reduce(card[win, g, t] & 255, axis=0)
            lead = win; rows.append(row); cards.append(card); wins.append(win)
        o = np.argsort(np.stack(wins) * K + np.arange(K)[:, None, None], axis=0)
        pile = np.take_along_axis(np.stack(cards), o[:, None], 0).reshape(N, K, 8, TB)
        for k in range(K):
            np.put_along_axis(c, rows[k], pile[:, k][..., None], 3)
            np.put_along_axis(e, rows[k], 0, 3)
        live = np.ones((N, 8, TB, 16), bool)
    return {"yc": np.stack([gtable(a.reshape(8, -1)) for a in c]).astype(np.float32), "yw": won.astype(np.float32)}

@@ -1,0 +1,726 @@
+from concourse.bass import DstId, RemoteDMATransfer
+from concourse.mybir import AluOpType as OP, AxisListType, ActivationFunctionType as AF
+
+NH = 3
+REP = 4
+SCH = 1
+Q = 2
+VGT = 1
+SPLIT = 0
+FUSED = "y"
+FAR2 = True
+STAG = 3000.0
+TOL = 30
+GC = 1.5
+W1 = 60
+W2 = 120
+PE = 0.6
+SEND = 700
+XLAT = 5000.0
+NS = 4
+TH = 12 // NH
+n = 16 * TH
+SL = ((6 - SPLIT) * TH + 3) // 4 * 4
+RS = NS * SL
+SP = (TH + 3) // 4 * 4
+KQ = 16 // Q
+M1R = ["i", "b", 0, 1, 2, 3, 4, 5]
+M2R = ["i", "b", 0, 1, 3, 4]
+SC = (4 * TH + 15) // 16
+YC = (REP * TH + 15) // 16
+F32, BF, I32, U16 = "float32", "bfloat16", "int32", "uint16"
+
+LISTS = [("e3", TH), ("eq2", TH), ("e15", TH), ("col", TH), ("perm", TH), ("K", TH), ("P", TH), ("yl", YC), ("sm", SC),
+         ("SS", TH), ("RD", TH), ("X3", 3 * TH), ("dup", 24), ("sel", 12)]
+LOFF = {}
+_o = 0
+for _k, _w in LISTS:
+    if _k != "eq2":
+        _o += _o % 2
+    LOFF[_k] = (_o, _o + _w)
+    _o += _w
+LW = _o + _o % 2
+
+_ALL = {
+    "book": (4096, BF), "hnd": (192, I32), "ldi": (192, I32), "ldb": (192, BF), "ldl": (16, F32), "z1": (384, F32),
+    "z2": (384, F32), "c0": (192, F32), "pi": (8, I32), "pf": (16, F32), "li": (LW, I32), "lt": (8, I32), "lu": (LW, U16),
+    "xr": (144, F32), "k16": (128, F32), "s4": (n, F32), "wb": (144, BF), "wc": (144, BF), "wt": (128, F32), "dg": (128, F32),
+    "i32": (128, F32), "in1": (128, F32), "i20": (128, BF), "i21": (128, BF), "i22": (128, BF), "one": (128, BF),
+    "cu": (2 * n, BF), "cb": (16, BF), "cg": (3 * n, BF), "ktb": (n, BF), "ktf": (n, F32), "kc": (n, F32), "r16": (n, F32),
+    "r4": (n, F32), "r4b": (n, F32), "r4d": (n, F32), "crd": (n, F32),
+}
+_PER = {
+    "m1": (len(M1R) * RS, I32), "m2": (len(M2R) * NS * n, BF), "m0": (6 * NS * SP, I32),
+    "cc": (2 * n, F32), "ck": (4 * n, F32), "cp": (2 * n, F32),
+    "ci": (2 * n, I32), "kk": (n, F32), "rw": (n, F32), "oh": (7 * n, F32), "aa": (n, F32), "nl": (16 * SC, F32),
+    "cq": (n, F32), "pr": (n, F32), "se": (8 * (n + 16), F32), "zi": (2 * n, I32), "of": (n, U16), "yu": (16 * YC + 16, U16),
+    "yr": (REP * n, BF), "eq": (2 * n, BF), "bs": (n, F32), "dd": (16 * n, BF), "ab": (32 * n, BF), "sg": (n, F32),
+    "tb": (n, F32), "ky": (2 * n, F32), "fp": (n, F32), "sc": (3 * n, F32), "no": (3 * n, BF), "o3": (3 * n, F32),
+    "nr": (n, F32), "sm": (48, I32), "ss": (64, F32), "x3": (5 * n, F32), "wn": (16, F32), "we": (n, BF), "wo": (n, F32),
+    "yo": (n, F32),
+}
+SCRATCH = {"pv": ("psum", [128, 512], F32)}
+for _k, (_w, _d) in _ALL.items():
+    SCRATCH[_k] = ("sbuf", [128, _w], _d)
+for _k, (_w, _d) in _PER.items():
+    SCRATCH[_k] = ("sbuf", [128, NH * ((_w + 15) // 16 * 16)], _d)
+UB = Q if NH * (Q + 1) <= 7 else 1
+for _h in range(NH):
+    SCRATCH["pm%d" % _h] = ("psum", [128, 512], F32)
+    for _u in range(UB):
+        SCRATCH["pu%d_%d" % (_h, _u)] = ("psum", [128, 512], F32)
+
+SEMAPHORES = (["V", "S", "P", "G", "sent", "dh", "db", "dl"] + ["dy%d" % h for h in range(NH)] + ["dw%d" % h for h in range(NH)]
+              + ["a%d_%s" % (h, r) for h in range(NH) for r in M1R] + ["y%d_%s" % (h, r) for h in range(NH) for r in M2R]
+              + ["p%d_%s" % (h, r) for h in range(NH) for r in range(6 * SPLIT)])
+
+
+def A(name, lo, hi, step=1, p0=0, p1=128):
+    return (name, lo, hi, step, p0, p1)
+
+
+def IND(win, off):
+    return ("*", win, off)
+
+
+def width(a):
+    if a[0] == "*":
+        return 16 * width(a[2])
+    return len(range(a[1], a[2], a[3]))
+
+
+def cols(a):
+    if a[3] == 1:
+        return ((1 << (a[2] - a[1])) - 1) << a[1]
+    m = 0
+    for c in range(a[1], a[2], a[3]):
+        m |= 1 << c
+    return m
+
+
+def two(a):
+    return SCRATCH[a[0]][2] in (BF, U16)
+
+
+def psum(a):
+    return a[0] != "*" and SCRATCH[a[0]][0] == "psum"
+
+
+def routes(T, topo, core):
+    near = [c for c in T.cores if c != core and topo.may_write(core, c)]
+    far = [c for c in T.cores if c != core and not topo.may_write(core, c)]
+    cand = [c for c in topo.cores_of(core) if c != core and all(topo.may_write(c, d) for d in far)]
+    cand.sort(key=lambda c: (topo.die(c) != topo.die(core), c))
+    r1 = cand[:len(far)]
+    r2 = cand[len(far):2 * len(far)] if FAR2 else r1
+    return near, far, r1, r2
+
+
+def shares(T, topo, core, kind):
+    near, far, r1, r2 = routes(T, topo, core)
+    es = topo.engines(core, r1[0])
+    if kind in FUSED:
+        es = [e for e in es if e not in topo.engines(core, near[0])]
+    k = len(es) // len(far)
+    return [es[x * k:(x + 1) * k] for x in range(len(far))]
+
+
+def bits(es):
+    m = 0
+    for e in es:
+        m |= 1 << e
+    return m
+
+
+def build(me):
+    ops = []
+    tag = [0]
+
+    def add(eng, what, reads, writes, busy, lat=None, sem=None, after=()):
+        rd = []
+        for a in reads:
+            if isinstance(a, tuple):
+                rd += [a[1], a[2]] if a[0] == "*" else [a]
+        ops.append({"eng": eng, "what": what, "rd": rd, "wr": list(writes), "busy": busy,
+                    "lat": busy if lat is None else lat, "sem": sem, "after": list(after), "h": tag[0]})
+        return len(ops) - 1
+
+    def vc(w, c, ind):
+        return 50 + GC * w if ind else max(64, w * c)
+
+    def tt(out, a, b, op):
+        add("V", ("tt", out, a, b, op), [a, b], [out], vc(width(out), 1 if psum(a) or psum(b) else 2, a[0] == "*"))
+
+    def ts(out, a, s1, s2, op0, op1=None):
+        ind = a[0] == "*"
+        add("V", ("ts", out, a, s1, s2, op0, op1), [a, s1, s2], [out],
+            vc(width(out), 0.5 if not ind and two(a) and two(out) else 1, ind))
+
+    def cp(out, a):
+        add("V", ("cp", out, a), [a], [out], vc(width(out), 1, a[0] == "*"))
+
+    def scan(out, d0, d1, op0, op1):
+        add("V", ("scan", out, d0, d1, op0, op1), [d0, d1], [out], vc(width(out), 1, False))
+
+    def ms(out, v):
+        add("V", ("ms", out, v), [], [out], vc(width(out), 1, False))
+
+    def tr(out, a):
+        add("V", ("tr", out, a), [a], [out], vc(width(out), 1, False))
+
+    def act(out, a, f, bias=0.0, scale=1.0):
+        add("S", ("act", out, a, f, bias, scale), [a], [out], 65 + GC * width(out) if a[0] == "*" else 60 + width(out))
+
+    def mm(items):
+        c = 0
+        for o, l, r, s0, s1 in items:
+            c += max(64, width(r)) * (4 * PE if SCRATCH[r[0]][2] == F32 else PE)
+        add("P", ("mm", items), [x for it in items for x in it[1:3]], [it[0] for it in items], c, c + 60)
+
+    def iota(out, pat, base, cm):
+        add("G", ("iota", out, pat, base, cm), [], [out], 130 + 2 * width(out))
+
+    def L(k, w=None):
+        lo, hi = LOFF[k]
+        return A("lu", lo, hi if w is None else lo + w)
+
+    def Li(k):
+        return A("li", LOFF[k][0], LOFF[k][1])
+
+    add("Y", ("dma", A("hnd", 0, 192), "hand", None), [], [A("hnd", 0, 192)], 60, 2200, "dh")
+    add("Y", ("dma", A("book", 0, 4096), "bk", None), [], [A("book", 0, 4096)], 60, 6000, "db")
+    add("S", ("dma", A("ldi", 0, 192, 1, 0, 8), "ld", None), [], [A("ldi", 0, 192)], 60, 2200, "dl")
+
+    def PI(i):
+        return A("pi", i, i + 1)
+
+    def PF(i):
+        return A("pf", i, i + 1)
+
+    def LT(i, w):
+        return A("lt", i, i + w)
+    iota(PI(0), [[1, 1]], 0, 1)
+    iota(Li("dup"), [[16, 12], [0, 2]], 0, 0)
+    iota(Li("sel"), [[32, 12]], 0, 0)
+    iota(A("kc", 0, n), [[0, TH], [-8192, 16]], 8192 * 15, 0)
+    ts(PI(1), PI(0), 15, None, OP.bitwise_and)
+    ts(PI(2), PI(0), 3, None, OP.bitwise_and)
+    ts(PI(3), PI(0), 2, 3, OP.arith_shift_right, OP.bitwise_and)
+    ts(PI(4), PI(0), 31, None, OP.bitwise_and)
+    ts(PI(5), PI(0), 112, None, OP.bitwise_and)
+    cp(A("pf", 0, 6), A("pi", 0, 6))
+    ts(L("dup"), Li("dup"), PF(1), None, OP.add)
+    ts(L("sel"), Li("sel"), PF(4), None, OP.add)
+
+    def turn(out, src, w, z0, addc):
+        if addc:
+            ts(A("z1", z0, z0 + 2 * w), IND(src, L("dup", w // 8)), addc, None, OP.add)
+        else:
+            cp(A("z1", z0, z0 + 2 * w), IND(src, L("dup", w // 8)))
+        tr(A("z2", z0, z0 + 2 * w), A("z1", z0, z0 + 2 * w))
+        cp(out, IND(A("z2", z0, z0 + 2 * w), L("sel", w // 16)))
+    turn(A("c0", 0, 192), A("hnd", 0, 192), 192, 0, 0)
+
+    iota(Li("col"), [[1, TH]], 0, 0)
+    iota(Li("e15"), [[16, TH]], 15, 0)
+    iota(Li("X3"), [[4, 3], [16, TH]], 3, 0)
+    iota(Li("yl"), [[16, YC]], 0, 0)
+    iota(Li("sm"), [[16, SC]], 0, 0)
+    iota(A("xr", 0, 144), [[1, 144]], 0, 0)
+    iota(A("k16", 0, 128), [[0, 8], [1, 16]], 0, 0)
+    iota(A("s4", 0, n), [[0, n // 4], [1, 4]], 0, 0)
+    cp(L("col"), Li("col"))
+    cp(L("e15"), Li("e15"))
+    cp(L("X3"), Li("X3"))
+    ts(L("eq2"), Li("col"), float(n), None, OP.add)
+    ts(L("e3"), Li("e15"), -12.0, None, OP.add)
+    ts(PF(6), PF(1), float(TH), None, OP.mult)
+    ts(L("perm"), Li("col"), PF(6), None, OP.add)
+    ts(PF(7), PF(2), float(SL), None, OP.mult)
+    ts(PF(13), PF(2), float(SP if SPLIT else SL), 0.0 if SPLIT else 5.0 * TH, OP.mult, OP.add)
+    ts(L("K"), Li("col"), PF(13), None, OP.add)
+    ts(PF(8), PF(3), float(TH), PF(7), OP.mult, OP.add)
+    ts(L("P"), Li("col"), PF(8), None, OP.add)
+    ts(PF(9), PF(2), float(TH), None, OP.mult)
+    ts(L("SS"), Li("col"), PF(9), None, OP.add)
+    ts(Li("yl"), Li("yl"), PF(1), None, OP.add)
+    ts(LT(0, YC), Li("yl"), 1.0 / TH, 0.5 / TH - 0.5, OP.mult, OP.add)
+    ts(LT(0, YC), LT(0, YC), float(-TH), None, OP.mult)
+    tt(LT(0, YC), LT(0, YC), Li("yl"), OP.add)
+    ts(L("yl"), LT(0, YC), 16.0, 7.0, OP.mult, OP.add)
+    ts(Li("sm"), Li("sm"), PF(1), None, OP.add)
+    ts(LT(4, SC), Li("sm"), 1.0 / TH, 0.5 / TH - 0.5, OP.mult, OP.add)
+    ts(LT(6, SC), LT(4, SC), float(-TH), None, OP.mult)
+    tt(LT(6, SC), LT(6, SC), Li("sm"), OP.add)
+    ts(LT(6, SC), LT(6, SC), 16.0, 15.0, OP.mult, OP.add)
+    ts(LT(4, SC), LT(4, SC), -1.0, None, OP.add)
+    tt(LT(4, SC), LT(4, SC), LT(4, SC), OP.mult)
+    ts(LT(4, SC), LT(4, SC), 2.0, float(n), OP.min, OP.mult)
+    tt(Li("sm"), LT(4, SC), LT(6, SC), OP.add)
+    cp(L("sm"), Li("sm"))
+    ts(PF(10), PF(5), 15.0, None, OP.add)
+    ts(A("wb", 0, 144), A("xr", 0, 144), PF(10), 64.0, OP.is_equal, OP.mult)
+    ts(PF(11), PF(0), 16.0, 15.0, OP.mult, OP.add)
+    ts(A("wc", 0, 144), A("xr", 0, 144), PF(11), None, OP.is_equal)
+    ts(A("wt", 0, 128), A("k16", 0, 128), PF(1), 416.0 / 2048, OP.is_equal, OP.mult)
+    ts(A("dg", 0, 128), A("k16", 0, 128), PF(1), None, OP.is_equal)
+    ts(A("i32", 0, 128), A("xr", 0, 128), PF(0), 32.0, OP.is_equal, OP.mult)
+    act(A("in1", 0, 128), A("i32", 0, 128), AF.Identity, 0.0, -1.0 / 32)
+    act(A("i20", 0, 128), A("i32", 0, 128), AF.Identity, 0.0, 32768.0)
+    act(A("i21", 0, 128), A("i32", 0, 128), AF.Identity, 0.0, 65536.0)
+    act(A("i22", 0, 128), A("i32", 0, 128), AF.Identity, 0.0, 131072.0)
+    ms(A("one", 0, 128), 1.0)
+    w2 = KQ * TH
+    ks = min(KQ, REP * SCH)
+    ms(A("cu", 0, 2 * n), -262144.0)
+    for k0 in range(0, 16, ks):
+        o = (k0 // KQ * 2 + 1) * w2 + k0 % KQ * TH
+        ms(A("cu", o, o + ks * TH), -1024.0 if k0 >= 16 - VGT * ks else 0.0)
+    ms(A("cb", 0, 16), -8388608.0)
+    for jj in range(3):
+        ms(A("cg", jj * n, (jj + 1) * n), 262144.0 * (1 - 16 * jj))
+    act(A("ktf", 0, n), A("k16", 0, n), AF.Identity, 60.0 + me, -4.0)
+    act(A("ktb", 0, n), A("k16", 0, n), AF.Identity, 60.0 + me, -4.0)
+    ts(A("r16", 0, n), A("k16", 0, n), 0.0, None, OP.not_equal)
+    ts(A("r4", 0, n), A("s4", 0, n), 0.0, None, OP.not_equal)
+    ts(A("r4b", 0, n), A("s4", 0, n), 0.0, 4194304.0, OP.is_equal, OP.mult)
+    cp(A("r4d", 0, n), A("r4", 0, n))
+    ms(A("r4d", 3, n, 4), -1.0)
+    cp(A("ldb", 0, 192, 1, 0, 8), A("ldi", 0, 192, 1, 0, 8))
+    mm([(A("pm0", 0, 12), A("wc", 15 - r, 143 - r, 1, 0, 8), A("ldb", r, 192, 16, 0, 8), r == 0, r == 15) for r in range(16)])
+    ms(A("ldl", 12, 16), 0.0)
+    cp(A("ldl", 0, 12), A("pm0", 0, 12))
+    ms(A("crd", 0, n), 0.0)
+    ms(A("x3", 0, 16), float(4 * TH))
+    for i in range(3):
+        pos, seat = (3 * me + i) // NS, (3 * me + i) % NS
+        for j, v in enumerate((2 - pos, pos - 1, pos)):
+            ms(A("crd", 4 * i + j, n, 16), float(v))
+            ms(A("x3", 4 * i + j, 4 * i + j + 1), float(j * RS + seat * SL + 4 * TH))
+        ms(A("x3", 4 * i + 3, 4 * i + 4), float(i * RS + me * SL + 4 * TH))
+    tt(A("x3", 16, 32), A("x3", 0, 16), A("dg", 0, 16), OP.mult)
+    add("V", ("red", PF(12), A("x3", 16, 32)), [A("x3", 16, 32)], [PF(12)], 64)
+    ts(L("RD"), Li("col"), PF(12), None, OP.add)
+    one = A("one", 0, 128, 1, 0, 1)
+
+    for h in range(NH):
+        def B(name, lo, hi, step=1, p0=0, p1=128):
+            o = h * ((_PER[name][0] + 15) // 16 * 16)
+            return A(name, o + lo, o + hi, step, p0, p1)
+        pm = "pm%d" % h
+        tag[0] = h
+
+        def m1(r, f0=0, f1=None, seat=me):
+            o = M1R.index(r) * RS + seat * SL
+            return B("m1", o + f0 * TH, o + (SL if f1 is None else f1 * TH))
+
+        def m0(r, seat=me, w=SP):
+            o = (r * NS + seat) * SP
+            return B("m0", o, o + w)
+
+        def m1w(r, k=1):
+            return B("m1", M1R.index(r) * RS, (M1R.index(r) + k) * RS)
+
+        def m2(r, seat=me):
+            o = (M2R.index(r) * NS + seat) * n
+            return B("m2", o, o + n)
+
+        def m2w(r):
+            return B("m2", M2R.index(r) * NS * n, (M2R.index(r) + 1) * NS * n)
+
+        def send(kind, r):
+            slot = {"a": m1, "y": m2, "p": m0}[kind]
+            sem = "%s%d_%s" % (kind, h, r)
+            s = add("G", ("send", kind, slot(r, seat=me), sem), [slot(r, seat=me)], [], SEND * (0.6 if kind in FUSED else 1))
+            add(None, ("arrive",), [], [slot(r, seat=q) for q in range(NS) if q != me], 0, XLAT - SEND, sem, [s])
+
+        def cc(d):
+            return B("cc", d * n, (d + 1) * n)
+
+        def ckp(d):
+            return B("cp", d * n, (d + 1) * n)
+
+        def ckl(d, lo=0, step=1):
+            return B("ck", (2 * d + 1) * n + lo, (2 * d + 2) * n, step)
+
+        def oh(j, lo=0, step=1):
+            return B("oh", j * n + lo, (j + 1) * n, step)
+
+        def se(j, lo=0, step=1, hi=n):
+            return B("se", j * (n + 16) + lo, j * (n + 16) + hi, step)
+
+        def no(jj):
+            return B("no", jj * n, (jj + 1) * n)
+
+        def suits(d):
+            cp(B("ci", 0, n), ckl(d))
+            ts(B("ci", n, 2 * n), B("ci", 0, n), 3, None, OP.bitwise_and)
+            cp(B("ck", 2 * d * n, (2 * d + 1) * n), B("ci", n, 2 * n))
+
+        def close(r, rec):
+            tt(B("sm", 0, 16 * SC), IND(B("sc", 0, 3 * n), L("sm")), B("nl", 0, 16 * SC), OP.mult)
+            ts(m1(r, 2, 6 - SPLIT), B("sm", 0, (4 - SPLIT) * TH), 0x7FFC3, None, OP.bitwise_and)
+            if rec:
+                ts(m1(r, 0, 1), B("sm", TH, 2 * TH), 6, 3, OP.arith_shift_right, OP.bitwise_and)
+            send("a", r)
+            if rec:
+                ts(B("yu", 16 * YC, 16 * YC + TH), m1(r, 3, 4), 1.0 / 64, -32.0, OP.mult, OP.add)
+                act(m2(r), IND(A("book", 0, 4096), B("yu", 16 * YC, 16 * YC + TH)), AF.Copy)
+                send("y", r)
+
+        def winner(j, r):
+            tt(B("kk", 0, n), IND(B("m0", r * NS * SP, (r + 1) * NS * SP) if SPLIT else m1w(r), L("K")), B("aa", 0, n), OP.add)
+            scan(B("rw", 0, n), A("r4b", 0, n), B("kk", 0, n), OP.add, OP.min)
+            tt(oh(j), IND(B("rw", 0, n), L("e3")), B("kk", 0, n), OP.is_equal)
+
+        def pick(j, slot, r):
+            tt(B("pr", 0, n), IND(m1w(r), L("P")), oh(j), OP.mult)
+            scan(se(slot), A("r4", 0, n), B("pr", 0, n), OP.mult, OP.add)
+
+        def redeal(d):
+            w = [se(3 * d + 1 + i, 7, 16) for i in range(3)]
+
+            def sa(i):
+                return B("ss", 32 + 8 * i, 32 + 8 * i + TH)
+            tt(sa(0), w[0], w[1], OP.is_le)
+            tt(sa(1), w[0], w[2], OP.is_le)
+            tt(sa(2), w[1], w[2], OP.is_le)
+            tt(B("ss", 0, TH), sa(0), sa(1), OP.add)
+            tt(B("ss", TH, 2 * TH), sa(0), sa(2), OP.subtract)
+            tt(B("ss", 2 * TH, 3 * TH), sa(1), sa(2), OP.add)
+            tt(B("kk", 0, n), IND(B("ss", 0, 4 * TH), L("SS")), A("crd", 0, n), OP.is_equal)
+            tt(B("pr", 0, n), IND(m1w(3 * d, 3), L("RD")), B("kk", 0, n), OP.mult)
+            scan(B("rw", 0, n), A("r4d", 0, n), B("pr", 0, n), OP.mult, OP.add)
+            tt(B("x3", 0, 3 * n), IND(B("rw", 0, n), L("X3")), B("o3", 0, 3 * n), OP.mult)
+            tt(B("x3", 3 * n, 4 * n), B("x3", 0, n), B("x3", n, 2 * n), OP.add)
+            tt(B("x3", 4 * n, 5 * n), ckl(0) if d == 0 else B("cq", 0, n), B("x3", 2 * n, 3 * n), OP.subtract)
+            tt(ckl(1) if d == 0 else B("x3", 0, n), B("x3", 4 * n, 5 * n), B("x3", 3 * n, 4 * n), OP.subtract)
+
+        c0 = A("c0", h * n, (h + 1) * n)
+        for r in M1R:
+            iota(m1(r, 0, 2), [[0, 2], [16, TH]], me * n, 1)
+            if SL > (6 - SPLIT) * TH:
+                ms(m1(r, 6 - SPLIT), 0)
+            if SPLIT and SP > TH and r in range(6):
+                ms(m0(r), 0)
+        ms(B("sc", 0, 3 * n), 0.0)
+        ms(B("nl", 0, 16 * SC), 64.0)
+        ms(B("nl", 0, TH), 2048.0)
+        tt(ckp(0), c0, A("kc", 0, n), OP.add)
+        ts(ckl(0), ckp(0), 32.0, None, OP.add)
+        cp(B("sc", 15, n, 16), ckl(0, 0, 16))
+        close("i", True)
+        act(cc(0), c0, AF.Identity, -32.0, 1.0 / 64)
+        suits(0)
+        ms(B("ss", 3 * TH, 4 * TH), 0.0)
+        ms(B("wn", 0, 16), 0.0)
+        for j in range(8):
+            ms(se(j, n, 1, n + 16), 0.0)
+        ts(B("yu", 0, TH), L("col"), float(h * TH), None, OP.add)
+        tt(oh(0), IND(A("ldl", 0, 16), B("yu", 0, TH)), A("s4", 0, n), OP.is_equal)
+
+        for j in range(7):
+            d, jj = j // 3, j % 3
+            if j > 0:
+                winner(j, j - 1)
+            pick(j, j, "i" if j == 0 else j - 1)
+            sl = j
+            if j == 6:
+                break
+            if j == 3:
+                redeal(0)
+                scan(B("sc", 0, n), B("nr", 0, n), ckl(1), OP.mult, OP.max)
+                close("b", True)
+                act(ckp(1), ckl(1), AF.Identity, -32.0)
+                tt(B("cq", 0, n), ckl(1), A("kc", 0, n), OP.subtract)
+                act(cc(1), B("cq", 0, n), AF.Identity, -32.5, 1.0 / 64)
+                suits(1)
+                pick(j, 7, "b")
+                sl = 7
+            ry = "i" if j == 0 else "b" if j == 3 else j - 1
+            mm([(A(pm, 0, TH), one, A("cb", 0, TH, 1, 0, 1), True, False)])
+            mm([(A(pm, 0, TH), A("wt", 0, 128), se(j, 11, 16), False, False),
+                (A(pm, 0, TH), A("i32", 0, 128), se(sl, 15, 16), False, True)])
+            o = cc(d)[1]
+            for th in range(TH):
+                ts(B("zi", th, n, TH), A("cc", o + 16 * th, o + 16 * th + 16), se(sl, 16 * th + 15, 1, 16 * th + 16),
+                   A(pm, th, th + 1), OP.mult, OP.add)
+            ts(B("zi", n, 2 * n), B("zi", 0, n), 5, 4095, OP.arith_shift_right, OP.bitwise_and)
+            cp(B("of", 0, n), B("zi", n, 2 * n))
+            ts(B("yu", 0, 16 * YC), IND(se(sl), L("yl")), PF(5), None, OP.subtract)
+            act(B("yr", 0, REP * n), IND(m2w(ry), B("yu", 0, REP * TH)), AF.Copy)
+            act(B("aa", 0, n), oh(j), AF.Identity, 0.0, 261760.0)
+            act(B("nl", 3 * TH, 4 * TH), oh(j, me, 16), AF.Identity, 1.0, -1.0)
+            tt(se(sl, n, 1, n + TH), oh(j, me, 16), B("sc", 15, n, 16), OP.mult)
+            tt(B("eq", 0, 2 * n), IND(se(sl, 0, 1, n + 16), A("lu", LOFF["e3"][0], LOFF["eq2"][1])),
+               B("ck", 2 * d * n, (2 * d + 2) * n), OP.is_equal)
+            pb = A(pm, 64, 64 + n)
+            mm([(pb, one, A("ktb", 0, n, 1, 0, 1), True, False)]
+               + [(pb, A("i22", 0, 128), no(i), False, False) for i in range(jj)])
+            mm([(pb, A("i20", 0, 128), B("eq", 0, n), False, False), (pb, A("i21", 0, 128), B("eq", n, 2 * n), False, True)])
+            act(B("bs", 0, n), pb, AF.Identity, 524288.0 - 4194304.0 * jj)
+            pg = A(pm, 256, 256 + n)
+            if j < 5:
+                mm([(pg, one, A("ktb", 0, n, 1, 0, 1), True, False),
+                    (pg, one, A("cg", jj * n, (jj + 1) * n, 1, 0, 1), False, False)]
+                   + [(pg, A("i22", 0, 128), no(i), False, False) for i in range(jj)])
+            for u in range(Q):
+                po = 0 if UB == Q else u * (512 // Q)
+                pu = A("pu%d_%d" % (h, u % UB), po, po + 2 * w2)
+                mm([(pu, one, A("cu", 2 * w2 * u, 2 * w2 * (u + 1), 1, 0, 1), True, False)])
+                for k0 in range(u * KQ, (u + 1) * KQ, ks):
+                    for k in range(k0, k0 + ks, REP):
+                        tt(B("dd", k * n, (k + REP) * n), IND(A("book", 0, 4096), B("of", k * TH, (k + REP) * TH)),
+                           B("yr", 0, REP * n), OP.subtract)
+                    a0 = 2 * u * KQ * n + (k0 - u * KQ) * n
+                    dd = B("dd", k0 * n, (k0 + ks) * n)
+                    act(B("ab", a0, a0 + ks * n), dd, AF.Abs)
+                    if k0 >= 16 - VGT * ks:
+                        ts(B("ab", a0 + KQ * n, a0 + (KQ + ks) * n), dd, 0.0, 2.0, OP.is_gt, OP.mult)
+                    else:
+                        act(B("ab", a0 + KQ * n, a0 + (KQ + ks) * n), dd, AF.Sign, -0.5)
+                mm([(pu, A("wb", 15 - r, 143 - r), B("ab", 2 * u * KQ * n + r, 2 * (u + 1) * KQ * n, 16),
+                     False, r == 15) for r in range(16)])
+            for u in range(Q):
+                pu = "pu%d_%d" % (h, u % UB)
+                po = 0 if UB == Q else u * (512 // Q)
+                act(B("sg", u * w2, (u + 1) * w2), A(pu, po + w2, po + 2 * w2), AF.Sign, 64.0, -1.0)
+                tt(B("tb", u * w2, (u + 1) * w2), B("sg", u * w2, (u + 1) * w2), A(pu, po, po + w2), OP.mult)
+            ky, k2 = B("ky", 0, n), B("ky", n, 2 * n)
+            tt(ky, IND(B("tb", 0, n), L("perm")), B("bs", 0, n), OP.add)
+            if j < 5:
+                act(B("fp", 0, n), IND(B("tb", 0, n), L("perm")), AF.Abs)
+                mm([(pg, A("in1", 0, 128), B("fp", 0, n), False, True)])
+            scan(B("sc", 2 * n, 3 * n), A("r16", 0, n), ky, OP.mult, OP.max)
+            if SPLIT:
+                tt(B("sm", 32, 32 + TH), B("sc", 2 * n + 15, 3 * n, 16), B("nl", 3 * TH, 4 * TH), OP.mult)
+                ts(m0(j, w=TH), B("sm", 32, 32 + TH), 0x7FFC3, None, OP.bitwise_and)
+                send("p", j)
+            tt(no(jj), IND(B("sc", 2 * n, 3 * n), L("e15")), ky, OP.not_equal)
+            scan(B("sc", n, 2 * n), no(jj), ckp(d), OP.mult, OP.max)
+            if jj == 2:
+                close(j, False)
+                act(B("o3", 0, 3 * n), B("no", 0, 3 * n), AF.Identity, 1.0 / 64, -1.0 / 64)
+            if j < 5:
+                tt(k2, no(jj), pg, OP.mult)
+                if jj == 2:
+                    tt(k2, k2, A("ktf", 0, n), OP.max)
+                pv = A("pv", h * n, (h + 1) * n)
+                scan(pv, A("r16", 0, n), k2, OP.mult, OP.max)
+                tt(B("nr", 0, n), k2, pv, OP.not_equal)
+                if jj < 2:
+                    scan(B("sc", 0, n), B("nr", 0, n), ckl(d), OP.mult, OP.max)
+                    close(j, True)
+        redeal(1)
+        turn(B("yo", 0, n), B("x3", 0, n), n, 2 * h * n, -32.0)
+        add("Y", ("out", "yc", h, B("yo", 0, n)), [B("yo", 0, n)], [], 60, 2200, "dy%d" % h)
+        mm([(A(pm, 0, TH), A("i32", 0, 128), oh(j, me, 16), j == 1, j == 6) for j in range(1, 7)])
+        act(B("wn", 0, TH), A(pm, 0, TH), AF.Identity, 0.0, 1.0 / 32)
+        tt(B("we", 0, n), IND(B("wn", 0, 16), L("col")), A("dg", 0, n), OP.mult)
+        mm([(A(pm, 64, 64 + n, 1, 0, 8), A("wb", 15, 143, 16), B("we", 0, n), True, True)])
+        act(B("wo", 0, n, 1, 0, 8), A(pm, 64, 64 + n, 1, 0, 8), AF.Identity, 0.0, 1.0 / 64)
+        add("S", ("out", "yw", h, B("wo", 0, n, 1, 0, 8)), [B("wo", 0, n)], [], 60, 2200, "dw%d" % h)
+    return ops
+
+
+def deps(ops):
+    hist, bank = {}, {}
+    for i, o in enumerate(ops):
+        dep = set(o["after"])
+        for a in o["rd"]:
+            m = cols(a)
+            dep.update(j for j, w, mk in hist.get(a[0], ()) if w and mk & m)
+        for a in o["wr"]:
+            m = cols(a)
+            dep.update(j for j, w, mk in hist.get(a[0], ()) if mk & m)
+        for b in sorted(set(a[0] for a in o["rd"] + o["wr"] if psum(a) and a[0] != "pv")):
+            e, cur, prev = bank.get(b, (None, [], []))
+            if e == o["eng"]:
+                dep.update(prev + (cur[-1:] if e == "P" else []))
+                bank[b] = (e, cur + [i], prev)
+            else:
+                dep.update(cur)
+                bank[b] = (o["eng"], [i], cur)
+        for a in o["wr"]:
+            m = cols(a)
+            hist[a[0]] = [(j, w, mk & ~m) for j, w, mk in hist.get(a[0], ()) if mk & ~m] + [(i, True, m)]
+        for a in o["rd"]:
+            if a[0] != "book":
+                hist.setdefault(a[0], []).append((i, False, cols(a)))
+        dep.discard(i)
+        o["dep"] = sorted(dep)
+    return ops
+
+
+PLAN = []
+
+
+def plan():
+    if PLAN:
+        return PLAN[0]
+    ops = deps(build(0))
+
+    def gap(j, i):
+        a, b = ops[j]["eng"], ops[i]["eng"]
+        return 0 if a == b == "P" or b is None else W1 if a == b else W2
+    N_ = len(ops)
+    succ = [[] for _ in ops]
+    for i, o in enumerate(ops):
+        for j in o["dep"]:
+            succ[j].append(i)
+    pri = [0.0] * N_
+    for i in range(N_ - 1, -1, -1):
+        pri[i] = ops[i]["lat"] + max([pri[k] + gap(i, k) for k in succ[i]] + [0])
+    pri = [p - STAG * o["h"] for p, o in zip(pri, ops)]
+    left = [len(o["dep"]) for o in ops]
+    rdy = [0.0] * N_
+    free = {}
+    pool = [i for i in range(N_) if not left[i]]
+    order = []
+    while pool:
+        t0 = min(max(rdy[i], free.get(ops[i]["eng"], 0)) for i in pool)
+        i = max((k for k in pool if max(rdy[k], free.get(ops[k]["eng"], 0)) <= t0 + TOL), key=lambda k: pri[k])
+        pool.remove(i)
+        o = ops[i]
+        st = max(rdy[i], free.get(o["eng"], 0))
+        if o["eng"]:
+            free[o["eng"]] = st + o["busy"]
+        o["t"] = st
+        order.append(i)
+        for k in succ[i]:
+            fin = st + (o["busy"] if o["eng"] == ops[k]["eng"] == "P" else o["lat"])
+            rdy[k] = max(rdy[k], fin + gap(i, k))
+            left[k] -= 1
+            if not left[k]:
+                pool.append(k)
+    PLAN.append((order, [o["t"] for o in ops]))
+    return PLAN[0]
+
+
+def messages(me):
+    ops = build(me)
+    return [ops[i]["what"] for i in plan()[0] if ops[i]["what"][0] == "send"]
+
+
+def rank_program(g, core, T, topo):
+    def ap(a):
+        if not isinstance(a, tuple):
+            return a
+        if a[0] == "*":
+            return ap(a[1]).indirect(ap(a[2]))
+        return T[a[0]][a[4]:a[5], a[1]:a[2]:a[3]] if a[3] != 1 else T[a[0]][a[4]:a[5], a[1]:a[2]]
+
+    me = T.rank_of(core)
+    if me is None:
+        for s, src in enumerate(T.cores):
+            if core not in topo.cores_of(src):
+                continue
+            near, far, r1, r2 = routes(T, topo, src)
+            if core not in r1 + r2:
+                continue
+            sent = 0
+            for _, kind, slot, sem in messages(s):
+                rl = r2 if kind == "y" else r1
+                if core in rl:
+                    dst = far[rl.index(core)]
+                    rid, pid = topo.addr(dst, core)
+                    g.wait_ge(T.sem[sem], len(shares(T, topo, src, kind)[rl.index(core)]))
+                    g.remote_dma(ap(slot), ap(slot), T.sem[sem], T.sem.sent, pid, rid, topo.mask(core, dst))
+                    sent += len(topo.engines(core, dst))
+            g.wait_ge(T.sem.sent, sent)
+        return
+
+    near, far, r1, r2 = routes(T, topo, core)
+    arrive = 0
+    for src in T.cores:
+        if src != core:
+            arrive += len(topo.engines(src if src in near else routes(T, topo, src)[2][0], core))
+    ops = deps(build(me))
+    order, when = plan()
+    queue = {"V": g.vector, "S": g.scalar, "P": g.tensor, "G": g, "Y": g.sync}
+    count = {"V": 0, "S": 0, "P": 0, "G": 0}
+    known = {e: {} for e in queue}
+    sent = 0
+    for i in order:
+        o = ops[i]
+        e, w = o["eng"], o["what"]
+        if e is None:
+            o["done"], o["clock"] = (o["sem"], arrive), {o["sem"]: arrive}
+            continue
+        q, kn = queue[e], known[e]
+        need = {}
+        for j in o["dep"]:
+            p = ops[j]
+            if p["done"] is None or e == p["eng"] == "P":
+                continue
+            if p["done"][1] > need.get(p["done"][0], (0, 0))[0]:
+                need[p["done"][0]] = (p["done"][1], j)
+        for s_, (v, j) in sorted(need.items(), key=lambda x: -when[x[1][1]]):
+            if kn.get(s_, 0) < v:
+                q.wait_ge(T.sem[s_], v)
+                for s2, v2 in ops[j]["clock"].items():
+                    kn[s2] = max(kn.get(s2, 0), v2)
+        ins = []
+        if w[0] == "tt":
+            ins = [q.tensor_tensor(ap(w[1]), ap(w[2]), ap(w[3]), w[4])]
+        elif w[0] == "ts":
+            if w[6] is None:
+                ins = [q.tensor_scalar(ap(w[1]), ap(w[2]), ap(w[3]), None, w[5])]
+            else:
+                ins = [q.tensor_scalar(ap(w[1]), ap(w[2]), ap(w[3]), ap(w[4]), w[5], w[6])]
+        elif w[0] == "cp":
+            ins = [q.tensor_copy(ap(w[1]), ap(w[2]))]
+        elif w[0] == "scan":
+            ins = [q.tensor_tensor_scan(ap(w[1]), ap(w[2]), ap(w[3]), 0.0, w[4], w[5])]
+        elif w[0] == "ms":
+            ins = [q.memset(ap(w[1]), w[2])]
+        elif w[0] == "tr":
+            ins = [q.transpose(ap(w[1]), ap(w[2]))]
+        elif w[0] == "red":
+            ins = [q.tensor_reduce(ap(w[1]), ap(w[2]), AxisListType.X, OP.add)]
+        elif w[0] == "act":
+            if w[3] == AF.Copy:
+                ins = [q.activation(ap(w[1]), ap(w[2]), w[3])]
+            else:
+                ins = [q.activation(ap(w[1]), ap(w[2]), w[3], bias=w[4], scale=w[5])]
+        elif w[0] == "mm":
+            ins = [q.matmul(ap(a), ap(b), ap(c), s0, s1) for a, b, c, s0, s1 in w[1]]
+        elif w[0] == "iota":
+            if SCRATCH[w[1][0]][2] == I32:
+                ins = [q.iota(ap(w[1]), w[2], w[3], w[4])]
+            else:
+                ins = [q.iota(ap(w[1]), w[2], w[3], w[4], allow_small_or_imprecise_dtypes=True)]
+        elif w[0] == "dma":
+            q.dma_start(ap(w[1]), T[w[2]][:]).then_inc(T.sem[o["sem"]], 16)
+        elif w[0] == "out":
+            q.dma_start(T[w[1]][:, w[2] * n:(w[2] + 1) * n], ap(w[3])).then_inc(T.sem[o["sem"]], 16)
+        elif w[0] == "send":
+            def transfer(c, es):
+                rid, pid = topo.addr(c, core)
+                return RemoteDMATransfer(dst_ids=[DstId(rid=rid, pnc=pid)], dma_engine_mask=bits(es),
+                                         remote_sem=T.sem[w[3]], src=ap(w[2]), dst=ap(w[2]))
+            sh = shares(T, topo, core, w[1])
+            trs = [transfer(c, es) for c, es in zip(r2 if w[1] == "y" else r1, sh)]
+            tr2 = [transfer(c, topo.engines(core, c)) for c in near]
+            for call in ([trs + tr2] if w[1] in FUSED else [trs, tr2]):
+                q.remote_dma_fused(call, local_sem=T.sem.sent)
+            sent += sum(len(es) for es in sh) + sum(len(topo.engines(core, c)) for c in near)
+        if w[0] == "send":
+            o["done"] = None
+        elif o["sem"]:
+            o["done"] = (o["sem"], 16)
+            o["clock"] = dict(kn)
+            o["clock"][o["sem"]] = 16
+        else:
+            for x in ins:
+                x.then_inc(T.sem[e], 1)
+                count[e] += 1
+            o["done"] = (e, count[e])
+            o["clock"] = dict(kn)
+            o["clock"][e] = count[e]
+    for e in "VSPG":
+        g.wait_ge(T.sem[e], count[e])
+    g.wait_ge(T.sem.sent, sent)
+    for h in range(NH):
+        g.wait_ge(T.sem["dy%d" % h], 16)
+        g.wait_ge(T.sem["dw%d" % h], 16)

@@ -6,17 +6,16 @@ REP = 4
 SCH = 1
 Q = 2
 VGT = 1
-SPLIT = 0
-FUSED = "y"
-FAR2 = True
-STAG = 3000.0
+SPLIT = 1
+FUSED = ""
+STAG = 4000.0
 TOL = 30
 GC = 1.5
-W1 = 60
-W2 = 120
+W1 = 190
+W2 = 200
 PE = 0.6
 SEND = 700
-XLAT = 5000.0
+XLAT = 5300.0
 NS = 4
 TH = 12 // NH
 n = 16 * TH
@@ -111,9 +110,7 @@ def routes(T, topo, core):
     far = [c for c in T.cores if c != core and not topo.may_write(core, c)]
     cand = [c for c in topo.cores_of(core) if c != core and all(topo.may_write(c, d) for d in far)]
     cand.sort(key=lambda c: (topo.die(c) != topo.die(core), c))
-    r1 = cand[:len(far)]
-    r2 = cand[len(far):2 * len(far)] if FAR2 else r1
-    return near, far, r1, r2
+    return near, far, cand[:len(far)], cand[len(far):2 * len(far)]
 
 
 def shares(T, topo, core, kind):
@@ -331,8 +328,16 @@ def build(me):
         def send(kind, r):
             slot = {"a": m1, "y": m2, "p": m0}[kind]
             sem = "%s%d_%s" % (kind, h, r)
-            s = add("G", ("send", kind, slot(r, seat=me), sem), [slot(r, seat=me)], [], SEND * (0.6 if kind in FUSED else 1))
-            add(None, ("arrive",), [], [slot(r, seat=q) for q in range(NS) if q != me], 0, XLAT - SEND, sem, [s])
+            far2 = kind == "y" or (r == "i" and h == 1)
+            if kind in FUSED:
+                parts = [("both", XLAT + 800)]
+            else:
+                parts = [("far", XLAT), ("near", XLAT / 2)]
+            way = []
+            for part, lat in parts:
+                s = add("G", ("send", kind, slot(r, seat=me), sem, part, far2), [slot(r, seat=me)], [], SEND / 2)
+                way.append(add(None, ("way",), [], [], 0, lat - SEND / 2, None, [s]))
+            add(None, ("arrive",), [], [slot(r, seat=q) for q in range(NS) if q != me], 0, 0, sem, way)
 
         def cc(d):
             return B("cc", d * n, (d + 1) * n)
@@ -599,7 +604,7 @@ def plan():
 
 def messages(me):
     ops = build(me)
-    return [ops[i]["what"] for i in plan()[0] if ops[i]["what"][0] == "send"]
+    return [ops[i]["what"] for i in plan()[0] if ops[i]["what"][0] == "send" and ops[i]["what"][4] != "near"]
 
 
 def rank_program(g, core, T, topo):
@@ -619,8 +624,8 @@ def rank_program(g, core, T, topo):
             if core not in r1 + r2:
                 continue
             sent = 0
-            for _, kind, slot, sem in messages(s):
-                rl = r2 if kind == "y" else r1
+            for _, kind, slot, sem, part, far2 in messages(s):
+                rl = r2 if far2 else r1
                 if core in rl:
                     dst = far[rl.index(core)]
                     rid, pid = topo.addr(dst, core)
@@ -645,7 +650,7 @@ def rank_program(g, core, T, topo):
         o = ops[i]
         e, w = o["eng"], o["what"]
         if e is None:
-            o["done"], o["clock"] = (o["sem"], arrive), {o["sem"]: arrive}
+            o["done"], o["clock"] = (o["sem"], arrive) if o["sem"] else None, {o["sem"]: arrive}
             continue
         q, kn = queue[e], known[e]
         need = {}
@@ -699,12 +704,10 @@ def rank_program(g, core, T, topo):
                 rid, pid = topo.addr(c, core)
                 return RemoteDMATransfer(dst_ids=[DstId(rid=rid, pnc=pid)], dma_engine_mask=bits(es),
                                          remote_sem=T.sem[w[3]], src=ap(w[2]), dst=ap(w[2]))
-            sh = shares(T, topo, core, w[1])
-            trs = [transfer(c, es) for c, es in zip(r2 if w[1] == "y" else r1, sh)]
-            tr2 = [transfer(c, topo.engines(core, c)) for c in near]
-            for call in ([trs + tr2] if w[1] in FUSED else [trs, tr2]):
-                q.remote_dma_fused(call, local_sem=T.sem.sent)
-            sent += sum(len(es) for es in sh) + sum(len(topo.engines(core, c)) for c in near)
+            to = list(zip(r2 if w[5] else r1, shares(T, topo, core, w[1]))) if w[4] != "near" else []
+            to += [(c, topo.engines(core, c)) for c in near] if w[4] != "far" else []
+            q.remote_dma_fused([transfer(c, es) for c, es in to], local_sem=T.sem.sent)
+            sent += sum(len(es) for c, es in to)
         if w[0] == "send":
             o["done"] = None
         elif o["sem"]:

@@ -3,23 +3,20 @@ from concourse.mybir import AluOpType as OP, AxisListType, ActivationFunctionTyp
 
 NH = 3
 REP = 4
-SCH = 1
 Q = 2
-VGT = 1
-SPLIT = 1
-FUSED = ""
-STAG = 4000.0
+VGT = 2
+STAG = 3800.0
 TOL = 30
 GC = 1.5
 W1 = 190
 W2 = 200
 PE = 0.6
 SEND = 700
-XLAT = 5300.0
+XLAT = 4200.0
 NS = 4
 TH = 12 // NH
 n = 16 * TH
-SL = ((6 - SPLIT) * TH + 3) // 4 * 4
+SL = (5 * TH + 3) // 4 * 4
 RS = NS * SL
 SP = (TH + 3) // 4 * 4
 KQ = 16 // Q
@@ -53,8 +50,8 @@ _PER = {
     "cc": (2 * n, F32), "ck": (4 * n, F32), "cp": (2 * n, F32),
     "ci": (2 * n, I32), "kk": (n, F32), "rw": (n, F32), "oh": (7 * n, F32), "aa": (n, F32), "nl": (16 * SC, F32),
     "cq": (n, F32), "pr": (n, F32), "se": (8 * (n + 16), F32), "zi": (2 * n, I32), "of": (n, U16), "yu": (16 * YC + 16, U16),
-    "yr": (REP * n, BF), "eq": (2 * n, BF), "bs": (n, F32), "dd": (16 * n, BF), "ab": (32 * n, BF), "sg": (n, F32),
-    "tb": (n, F32), "ky": (2 * n, F32), "fp": (n, F32), "sc": (3 * n, F32), "no": (3 * n, BF), "o3": (3 * n, F32),
+    "yr": (REP * n, BF), "eq": (2 * n, BF), "bs": (n, F32), "dd": (16 * n, BF), "ab": (32 * n, BF), "sg": (2 * n, F32),
+    "tb": (2 * n, F32), "ky": (2 * n, F32), "fp": (n, F32), "sc": (3 * n, F32), "no": (3 * n, BF), "o3": (3 * n, F32),
     "nr": (n, F32), "sm": (48, I32), "ss": (64, F32), "x3": (5 * n, F32), "wn": (16, F32), "we": (n, BF), "wo": (n, F32),
     "yo": (n, F32),
 }
@@ -63,15 +60,13 @@ for _k, (_w, _d) in _ALL.items():
     SCRATCH[_k] = ("sbuf", [128, _w], _d)
 for _k, (_w, _d) in _PER.items():
     SCRATCH[_k] = ("sbuf", [128, NH * ((_w + 15) // 16 * 16)], _d)
-UB = Q if NH * (Q + 1) <= 7 else 1
 for _h in range(NH):
     SCRATCH["pm%d" % _h] = ("psum", [128, 512], F32)
-    for _u in range(UB):
-        SCRATCH["pu%d_%d" % (_h, _u)] = ("psum", [128, 512], F32)
+    SCRATCH["pu%d" % _h] = ("psum", [128, 512], F32)
 
 SEMAPHORES = (["V", "S", "P", "G", "sent", "dh", "db", "dl"] + ["dy%d" % h for h in range(NH)] + ["dw%d" % h for h in range(NH)]
               + ["a%d_%s" % (h, r) for h in range(NH) for r in M1R] + ["y%d_%s" % (h, r) for h in range(NH) for r in M2R]
-              + ["p%d_%s" % (h, r) for h in range(NH) for r in range(6 * SPLIT)])
+              + ["p%d_%s" % (h, r) for h in range(NH) for r in range(6)])
 
 
 def A(name, lo, hi, step=1, p0=0, p1=128):
@@ -113,11 +108,9 @@ def routes(T, topo, core):
     return near, far, cand[:len(far)], cand[len(far):2 * len(far)]
 
 
-def shares(T, topo, core, kind):
+def shares(T, topo, core):
     near, far, r1, r2 = routes(T, topo, core)
     es = topo.engines(core, r1[0])
-    if kind in FUSED:
-        es = [e for e in es if e not in topo.engines(core, near[0])]
     k = len(es) // len(far)
     return [es[x * k:(x + 1) * k] for x in range(len(far))]
 
@@ -232,9 +225,10 @@ def build(me):
     ts(L("eq2"), Li("col"), float(n), None, OP.add)
     ts(L("e3"), Li("e15"), -12.0, None, OP.add)
     ts(PF(6), PF(1), float(TH), None, OP.mult)
-    ts(L("perm"), Li("col"), PF(6), None, OP.add)
+    ts(PF(14), PF(1), float(KQ), float(KQ * TH), OP.is_ge, OP.mult)
+    ts(L("perm"), Li("col"), PF(6), PF(14), OP.add, OP.add)
     ts(PF(7), PF(2), float(SL), None, OP.mult)
-    ts(PF(13), PF(2), float(SP if SPLIT else SL), 0.0 if SPLIT else 5.0 * TH, OP.mult, OP.add)
+    ts(PF(13), PF(2), float(SP), None, OP.mult)
     ts(L("K"), Li("col"), PF(13), None, OP.add)
     ts(PF(8), PF(3), float(TH), PF(7), OP.mult, OP.add)
     ts(L("P"), Li("col"), PF(8), None, OP.add)
@@ -268,11 +262,10 @@ def build(me):
     act(A("i22", 0, 128), A("i32", 0, 128), AF.Identity, 0.0, 131072.0)
     ms(A("one", 0, 128), 1.0)
     w2 = KQ * TH
-    ks = min(KQ, REP * SCH)
     ms(A("cu", 0, 2 * n), -262144.0)
-    for k0 in range(0, 16, ks):
+    for k0 in range(0, 16, REP):
         o = (k0 // KQ * 2 + 1) * w2 + k0 % KQ * TH
-        ms(A("cu", o, o + ks * TH), -1024.0 if k0 >= 16 - VGT * ks else 0.0)
+        ms(A("cu", o, o + REP * TH), -1024.0 if k0 >= 16 - VGT * REP else 0.0)
     ms(A("cb", 0, 16), -8388608.0)
     for jj in range(3):
         ms(A("cg", jj * n, (jj + 1) * n), 262144.0 * (1 - 16 * jj))
@@ -304,7 +297,7 @@ def build(me):
         def B(name, lo, hi, step=1, p0=0, p1=128):
             o = h * ((_PER[name][0] + 15) // 16 * 16)
             return A(name, o + lo, o + hi, step, p0, p1)
-        pm = "pm%d" % h
+        pm, pu = "pm%d" % h, "pu%d" % h
         tag[0] = h
 
         def m1(r, f0=0, f1=None, seat=me):
@@ -329,12 +322,8 @@ def build(me):
             slot = {"a": m1, "y": m2, "p": m0}[kind]
             sem = "%s%d_%s" % (kind, h, r)
             far2 = kind == "y" or (r == "i" and h == 1)
-            if kind in FUSED:
-                parts = [("both", XLAT + 800)]
-            else:
-                parts = [("far", XLAT), ("near", XLAT / 2)]
             way = []
-            for part, lat in parts:
+            for part, lat in (("far", XLAT), ("near", XLAT / 2)):
                 s = add("G", ("send", kind, slot(r, seat=me), sem, part, far2), [slot(r, seat=me)], [], SEND / 2)
                 way.append(add(None, ("way",), [], [], 0, lat - SEND / 2, None, [s]))
             add(None, ("arrive",), [], [slot(r, seat=q) for q in range(NS) if q != me], 0, 0, sem, way)
@@ -364,7 +353,7 @@ def build(me):
 
         def close(r, rec):
             tt(B("sm", 0, 16 * SC), IND(B("sc", 0, 3 * n), L("sm")), B("nl", 0, 16 * SC), OP.mult)
-            ts(m1(r, 2, 6 - SPLIT), B("sm", 0, (4 - SPLIT) * TH), 0x7FFC3, None, OP.bitwise_and)
+            ts(m1(r, 2, 5), B("sm", 0, 3 * TH), 0x7FFC3, None, OP.bitwise_and)
             if rec:
                 ts(m1(r, 0, 1), B("sm", TH, 2 * TH), 6, 3, OP.arith_shift_right, OP.bitwise_and)
             send("a", r)
@@ -374,7 +363,7 @@ def build(me):
                 send("y", r)
 
         def winner(j, r):
-            tt(B("kk", 0, n), IND(B("m0", r * NS * SP, (r + 1) * NS * SP) if SPLIT else m1w(r), L("K")), B("aa", 0, n), OP.add)
+            tt(B("kk", 0, n), IND(B("m0", r * NS * SP, (r + 1) * NS * SP), L("K")), B("aa", 0, n), OP.add)
             scan(B("rw", 0, n), A("r4b", 0, n), B("kk", 0, n), OP.add, OP.min)
             tt(oh(j), IND(B("rw", 0, n), L("e3")), B("kk", 0, n), OP.is_equal)
 
@@ -404,9 +393,9 @@ def build(me):
         c0 = A("c0", h * n, (h + 1) * n)
         for r in M1R:
             iota(m1(r, 0, 2), [[0, 2], [16, TH]], me * n, 1)
-            if SL > (6 - SPLIT) * TH:
-                ms(m1(r, 6 - SPLIT), 0)
-            if SPLIT and SP > TH and r in range(6):
+            if SL > 5 * TH:
+                ms(m1(r, 5), 0)
+            if SP > TH and r in range(6):
                 ms(m0(r), 0)
         ms(B("sc", 0, 3 * n), 0.0)
         ms(B("nl", 0, 16 * SC), 64.0)
@@ -470,37 +459,31 @@ def build(me):
                     (pg, one, A("cg", jj * n, (jj + 1) * n, 1, 0, 1), False, False)]
                    + [(pg, A("i22", 0, 128), no(i), False, False) for i in range(jj)])
             for u in range(Q):
-                po = 0 if UB == Q else u * (512 // Q)
-                pu = A("pu%d_%d" % (h, u % UB), po, po + 2 * w2)
-                mm([(pu, one, A("cu", 2 * w2 * u, 2 * w2 * (u + 1), 1, 0, 1), True, False)])
-                for k0 in range(u * KQ, (u + 1) * KQ, ks):
-                    for k in range(k0, k0 + ks, REP):
-                        tt(B("dd", k * n, (k + REP) * n), IND(A("book", 0, 4096), B("of", k * TH, (k + REP) * TH)),
-                           B("yr", 0, REP * n), OP.subtract)
+                ps = A(pu, 2 * w2 * u, 2 * w2 * (u + 1))
+                mm([(ps, one, A("cu", 2 * w2 * u, 2 * w2 * (u + 1), 1, 0, 1), True, False)])
+                for k0 in range(u * KQ, (u + 1) * KQ, REP):
+                    dd = B("dd", k0 * n, (k0 + REP) * n)
+                    tt(dd, IND(A("book", 0, 4096), B("of", k0 * TH, (k0 + REP) * TH)), B("yr", 0, REP * n), OP.subtract)
                     a0 = 2 * u * KQ * n + (k0 - u * KQ) * n
-                    dd = B("dd", k0 * n, (k0 + ks) * n)
-                    act(B("ab", a0, a0 + ks * n), dd, AF.Abs)
-                    if k0 >= 16 - VGT * ks:
-                        ts(B("ab", a0 + KQ * n, a0 + (KQ + ks) * n), dd, 0.0, 2.0, OP.is_gt, OP.mult)
+                    act(B("ab", a0, a0 + REP * n), dd, AF.Abs)
+                    if k0 >= 16 - VGT * REP:
+                        ts(B("ab", a0 + KQ * n, a0 + (KQ + REP) * n), dd, 0.0, 2.0, OP.is_gt, OP.mult)
                     else:
-                        act(B("ab", a0 + KQ * n, a0 + (KQ + ks) * n), dd, AF.Sign, -0.5)
-                mm([(pu, A("wb", 15 - r, 143 - r), B("ab", 2 * u * KQ * n + r, 2 * (u + 1) * KQ * n, 16),
+                        act(B("ab", a0 + KQ * n, a0 + (KQ + REP) * n), dd, AF.Sign, -0.5)
+                mm([(ps, A("wb", 15 - r, 143 - r), B("ab", 2 * u * KQ * n + r, 2 * (u + 1) * KQ * n, 16),
                      False, r == 15) for r in range(16)])
-            for u in range(Q):
-                pu = "pu%d_%d" % (h, u % UB)
-                po = 0 if UB == Q else u * (512 // Q)
-                act(B("sg", u * w2, (u + 1) * w2), A(pu, po + w2, po + 2 * w2), AF.Sign, 64.0, -1.0)
-                tt(B("tb", u * w2, (u + 1) * w2), B("sg", u * w2, (u + 1) * w2), A(pu, po, po + w2), OP.mult)
+            act(B("sg", 0, 3 * w2), A(pu, w2, 4 * w2), AF.Sign, 64.0, -1.0)
+            tb = B("tb", 0, 3 * w2)
+            tt(tb, B("sg", 0, 3 * w2), A(pu, 0, 3 * w2), OP.mult)
             ky, k2 = B("ky", 0, n), B("ky", n, 2 * n)
-            tt(ky, IND(B("tb", 0, n), L("perm")), B("bs", 0, n), OP.add)
+            tt(ky, IND(tb, L("perm")), B("bs", 0, n), OP.add)
             if j < 5:
-                act(B("fp", 0, n), IND(B("tb", 0, n), L("perm")), AF.Abs)
+                act(B("fp", 0, n), IND(tb, L("perm")), AF.Abs)
                 mm([(pg, A("in1", 0, 128), B("fp", 0, n), False, True)])
             scan(B("sc", 2 * n, 3 * n), A("r16", 0, n), ky, OP.mult, OP.max)
-            if SPLIT:
-                tt(B("sm", 32, 32 + TH), B("sc", 2 * n + 15, 3 * n, 16), B("nl", 3 * TH, 4 * TH), OP.mult)
-                ts(m0(j, w=TH), B("sm", 32, 32 + TH), 0x7FFC3, None, OP.bitwise_and)
-                send("p", j)
+            tt(B("sm", 32, 32 + TH), B("sc", 2 * n + 15, 3 * n, 16), B("nl", 3 * TH, 4 * TH), OP.mult)
+            ts(m0(j, w=TH), B("sm", 32, 32 + TH), 0x7FFC3, None, OP.bitwise_and)
+            send("p", j)
             tt(no(jj), IND(B("sc", 2 * n, 3 * n), L("e15")), ky, OP.not_equal)
             scan(B("sc", n, 2 * n), no(jj), ckp(d), OP.mult, OP.max)
             if jj == 2:
@@ -604,7 +587,7 @@ def plan():
 
 def messages(me):
     ops = build(me)
-    return [ops[i]["what"] for i in plan()[0] if ops[i]["what"][0] == "send" and ops[i]["what"][4] != "near"]
+    return [ops[i]["what"] for i in plan()[0] if ops[i]["what"][0] == "send" and ops[i]["what"][4] == "far"]
 
 
 def rank_program(g, core, T, topo):
@@ -629,7 +612,7 @@ def rank_program(g, core, T, topo):
                 if core in rl:
                     dst = far[rl.index(core)]
                     rid, pid = topo.addr(dst, core)
-                    g.wait_ge(T.sem[sem], len(shares(T, topo, src, kind)[rl.index(core)]))
+                    g.wait_ge(T.sem[sem], len(shares(T, topo, src)[rl.index(core)]))
                     g.remote_dma(ap(slot), ap(slot), T.sem[sem], T.sem.sent, pid, rid, topo.mask(core, dst))
                     sent += len(topo.engines(core, dst))
             g.wait_ge(T.sem.sent, sent)
@@ -704,8 +687,10 @@ def rank_program(g, core, T, topo):
                 rid, pid = topo.addr(c, core)
                 return RemoteDMATransfer(dst_ids=[DstId(rid=rid, pnc=pid)], dma_engine_mask=bits(es),
                                          remote_sem=T.sem[w[3]], src=ap(w[2]), dst=ap(w[2]))
-            to = list(zip(r2 if w[5] else r1, shares(T, topo, core, w[1]))) if w[4] != "near" else []
-            to += [(c, topo.engines(core, c)) for c in near] if w[4] != "far" else []
+            if w[4] == "far":
+                to = list(zip(r2 if w[5] else r1, shares(T, topo, core)))
+            else:
+                to = [(c, topo.engines(core, c)) for c in near]
             q.remote_dma_fused([transfer(c, es) for c, es in to], local_sem=T.sem.sent)
             sent += sum(len(es) for c, es in to)
         if w[0] == "send":

from concourse.bass import DstId, RemoteDMATransfer
from concourse.mybir import AluOpType as OP, AxisListType, ActivationFunctionType as AF

NH = 3
REP = 4
Q = 2
VGT = 2
STAG = 3800.0
TOL = 30
GC = 1.5
W1 = 190
W2 = 200
PE = 0.6
SEND = 700
XLAT = 4200.0
NS = 4
TH = 12 // NH
n = 16 * TH
SL = (5 * TH + 3) // 4 * 4
RS = NS * SL
SP = (TH + 3) // 4 * 4
KQ = 16 // Q
M1R = ["i", "b", 0, 1, 2, 3, 4, 5]
M2R = ["i", "b", 0, 1, 3, 4]
SC = (4 * TH + 15) // 16
YC = (REP * TH + 15) // 16
F32, BF, I32, U16 = "float32", "bfloat16", "int32", "uint16"

LISTS = [("e3", TH), ("eq2", TH), ("e15", TH), ("col", TH), ("perm", TH), ("K", TH), ("P", TH), ("yl", YC), ("sm", SC),
         ("SS", TH), ("RD", TH), ("X3", 3 * TH), ("dup", 24), ("sel", 12)]
LOFF = {}
_o = 0
for _k, _w in LISTS:
    if _k != "eq2":
        _o += _o % 2
    LOFF[_k] = (_o, _o + _w)
    _o += _w
LW = _o + _o % 2

_ALL = {
    "book": (4096, BF), "hnd": (192, I32), "ldi": (192, I32), "ldb": (192, BF), "ldl": (16, F32), "z1": (384, F32),
    "z2": (384, F32), "c0": (192, F32), "pi": (8, I32), "pf": (16, F32), "li": (LW, I32), "lt": (8, I32), "lu": (LW, U16),
    "xr": (144, F32), "k16": (128, F32), "s4": (n, F32), "wb": (144, BF), "wc": (144, BF), "wt": (128, F32), "dg": (128, F32),
    "i32": (128, F32), "in1": (128, F32), "i20": (128, BF), "i21": (128, BF), "i22": (128, BF), "one": (128, BF),
    "cu": (2 * n, BF), "cb": (16, BF), "cg": (3 * n, BF), "ktb": (n, BF), "ktf": (n, F32), "kc": (n, F32), "r16": (n, F32),
    "r4": (n, F32), "r4b": (n, F32), "r4d": (n, F32), "crd": (n, F32),
}
_PER = {
    "m1": (len(M1R) * RS, I32), "m2": (len(M2R) * NS * n, BF), "m0": (6 * NS * SP, I32),
    "cc": (2 * n, F32), "ck": (4 * n, F32), "cp": (2 * n, F32),
    "ci": (2 * n, I32), "kk": (n, F32), "rw": (n, F32), "oh": (7 * n, F32), "aa": (n, F32), "nl": (16 * SC, F32),
    "cq": (n, F32), "pr": (n, F32), "se": (8 * (n + 16), F32), "zi": (2 * n, I32), "of": (n, U16), "yu": (16 * YC + 16, U16),
    "yr": (REP * n, BF), "eq": (2 * n, BF), "bs": (n, F32), "dd": (16 * n, BF), "ab": (32 * n, BF), "sg": (2 * n, F32),
    "tb": (2 * n, F32), "ky": (2 * n, F32), "fp": (n, F32), "sc": (3 * n, F32), "no": (3 * n, BF), "o3": (3 * n, F32),
    "nr": (n, F32), "sm": (48, I32), "ss": (64, F32), "x3": (5 * n, F32), "wn": (16, F32), "we": (n, BF), "wo": (n, F32),
    "yo": (n, F32),
}
SCRATCH = {"pv": ("psum", [128, 512], F32)}
for _k, (_w, _d) in _ALL.items():
    SCRATCH[_k] = ("sbuf", [128, _w], _d)
for _k, (_w, _d) in _PER.items():
    SCRATCH[_k] = ("sbuf", [128, NH * ((_w + 15) // 16 * 16)], _d)
for _h in range(NH):
    SCRATCH["pm%d" % _h] = ("psum", [128, 512], F32)
    SCRATCH["pu%d" % _h] = ("psum", [128, 512], F32)

SEMAPHORES = (["V", "S", "P", "G", "sent", "dh", "db", "dl"] + ["dy%d" % h for h in range(NH)] + ["dw%d" % h for h in range(NH)]
              + ["a%d_%s" % (h, r) for h in range(NH) for r in M1R] + ["y%d_%s" % (h, r) for h in range(NH) for r in M2R]
              + ["p%d_%s" % (h, r) for h in range(NH) for r in range(6)])


def A(name, lo, hi, step=1, p0=0, p1=128):
    return (name, lo, hi, step, p0, p1)


def IND(win, off):
    return ("*", win, off)


def width(a):
    if a[0] == "*":
        return 16 * width(a[2])
    return len(range(a[1], a[2], a[3]))


def cols(a):
    if a[3] == 1:
        return ((1 << (a[2] - a[1])) - 1) << a[1]
    m = 0
    for c in range(a[1], a[2], a[3]):
        m |= 1 << c
    return m


def two(a):
    return SCRATCH[a[0]][2] in (BF, U16)


def psum(a):
    return a[0] != "*" and SCRATCH[a[0]][0] == "psum"


def routes(T, topo, core):
    near = [c for c in T.cores if c != core and topo.may_write(core, c)]
    far = [c for c in T.cores if c != core and not topo.may_write(core, c)]
    cand = [c for c in topo.cores_of(core) if c != core and all(topo.may_write(c, d) for d in far)]
    cand.sort(key=lambda c: (topo.die(c) != topo.die(core), c))
    return near, far, cand[:len(far)], cand[len(far):2 * len(far)]


def shares(T, topo, core):
    near, far, r1, r2 = routes(T, topo, core)
    es = topo.engines(core, r1[0])
    k = len(es) // len(far)
    return [es[x * k:(x + 1) * k] for x in range(len(far))]


def bits(es):
    m = 0
    for e in es:
        m |= 1 << e
    return m


def build(me):
    ops = []
    tag = [0]

    def add(eng, what, reads, writes, busy, lat=None, sem=None, after=()):
        rd = []
        for a in reads:
            if isinstance(a, tuple):
                rd += [a[1], a[2]] if a[0] == "*" else [a]
        ops.append({"eng": eng, "what": what, "rd": rd, "wr": list(writes), "busy": busy,
                    "lat": busy if lat is None else lat, "sem": sem, "after": list(after), "h": tag[0]})
        return len(ops) - 1

    def vc(w, c, ind):
        return 50 + GC * w if ind else max(64, w * c)

    def tt(out, a, b, op):
        add("V", ("tt", out, a, b, op), [a, b], [out], vc(width(out), 1 if psum(a) or psum(b) else 2, a[0] == "*"))

    def ts(out, a, s1, s2, op0, op1=None):
        ind = a[0] == "*"
        add("V", ("ts", out, a, s1, s2, op0, op1), [a, s1, s2], [out],
            vc(width(out), 0.5 if not ind and two(a) and two(out) else 1, ind))

    def cp(out, a):
        add("V", ("cp", out, a), [a], [out], vc(width(out), 1, a[0] == "*"))

    def scan(out, d0, d1, op0, op1):
        add("V", ("scan", out, d0, d1, op0, op1), [d0, d1], [out], vc(width(out), 1, False))

    def ms(out, v):
        add("V", ("ms", out, v), [], [out], vc(width(out), 1, False))

    def tr(out, a):
        add("V", ("tr", out, a), [a], [out], vc(width(out), 1, False))

    def act(out, a, f, bias=0.0, scale=1.0):
        add("S", ("act", out, a, f, bias, scale), [a], [out], 65 + GC * width(out) if a[0] == "*" else 60 + width(out))

    def mm(items):
        c = 0
        for o, l, r, s0, s1 in items:
            c += max(64, width(r)) * (4 * PE if SCRATCH[r[0]][2] == F32 else PE)
        add("P", ("mm", items), [x for it in items for x in it[1:3]], [it[0] for it in items], c, c + 60)

    def iota(out, pat, base, cm):
        add("G", ("iota", out, pat, base, cm), [], [out], 130 + 2 * width(out))

    def L(k, w=None):
        lo, hi = LOFF[k]
        return A("lu", lo, hi if w is None else lo + w)

    def Li(k):
        return A("li", LOFF[k][0], LOFF[k][1])

    add("Y", ("dma", A("hnd", 0, 192), "hand", None), [], [A("hnd", 0, 192)], 60, 2200, "dh")
    add("Y", ("dma", A("book", 0, 4096), "bk", None), [], [A("book", 0, 4096)], 60, 6000, "db")
    add("S", ("dma", A("ldi", 0, 192, 1, 0, 8), "ld", None), [], [A("ldi", 0, 192)], 60, 2200, "dl")

    def PI(i):
        return A("pi", i, i + 1)

    def PF(i):
        return A("pf", i, i + 1)

    def LT(i, w):
        return A("lt", i, i + w)
    iota(PI(0), [[1, 1]], 0, 1)
    iota(Li("dup"), [[16, 12], [0, 2]], 0, 0)
    iota(Li("sel"), [[32, 12]], 0, 0)
    iota(A("kc", 0, n), [[0, TH], [-8192, 16]], 8192 * 15, 0)
    ts(PI(1), PI(0), 15, None, OP.bitwise_and)
    ts(PI(2), PI(0), 3, None, OP.bitwise_and)
    ts(PI(3), PI(0), 2, 3, OP.arith_shift_right, OP.bitwise_and)
    ts(PI(4), PI(0), 31, None, OP.bitwise_and)
    ts(PI(5), PI(0), 112, None, OP.bitwise_and)
    cp(A("pf", 0, 6), A("pi", 0, 6))
    ts(L("dup"), Li("dup"), PF(1), None, OP.add)
    ts(L("sel"), Li("sel"), PF(4), None, OP.add)

    def turn(out, src, w, z0, addc):
        if addc:
            ts(A("z1", z0, z0 + 2 * w), IND(src, L("dup", w // 8)), addc, None, OP.add)
        else:
            cp(A("z1", z0, z0 + 2 * w), IND(src, L("dup", w // 8)))
        tr(A("z2", z0, z0 + 2 * w), A("z1", z0, z0 + 2 * w))
        cp(out, IND(A("z2", z0, z0 + 2 * w), L("sel", w // 16)))
    turn(A("c0", 0, 192), A("hnd", 0, 192), 192, 0, 0)

    iota(Li("col"), [[1, TH]], 0, 0)
    iota(Li("e15"), [[16, TH]], 15, 0)
    iota(Li("X3"), [[4, 3], [16, TH]], 3, 0)
    iota(Li("yl"), [[16, YC]], 0, 0)
    iota(Li("sm"), [[16, SC]], 0, 0)
    iota(A("xr", 0, 144), [[1, 144]], 0, 0)
    iota(A("k16", 0, 128), [[0, 8], [1, 16]], 0, 0)
    iota(A("s4", 0, n), [[0, n // 4], [1, 4]], 0, 0)
    cp(L("col"), Li("col"))
    cp(L("e15"), Li("e15"))
    cp(L("X3"), Li("X3"))
    ts(L("eq2"), Li("col"), float(n), None, OP.add)
    ts(L("e3"), Li("e15"), -12.0, None, OP.add)
    ts(PF(6), PF(1), float(TH), None, OP.mult)
    ts(PF(14), PF(1), float(KQ), float(KQ * TH), OP.is_ge, OP.mult)
    ts(L("perm"), Li("col"), PF(6), PF(14), OP.add, OP.add)
    ts(PF(7), PF(2), float(SL), None, OP.mult)
    ts(PF(13), PF(2), float(SP), None, OP.mult)
    ts(L("K"), Li("col"), PF(13), None, OP.add)
    ts(PF(8), PF(3), float(TH), PF(7), OP.mult, OP.add)
    ts(L("P"), Li("col"), PF(8), None, OP.add)
    ts(PF(9), PF(2), float(TH), None, OP.mult)
    ts(L("SS"), Li("col"), PF(9), None, OP.add)
    ts(Li("yl"), Li("yl"), PF(1), None, OP.add)
    ts(LT(0, YC), Li("yl"), 1.0 / TH, 0.5 / TH - 0.5, OP.mult, OP.add)
    ts(LT(0, YC), LT(0, YC), float(-TH), None, OP.mult)
    tt(LT(0, YC), LT(0, YC), Li("yl"), OP.add)
    ts(L("yl"), LT(0, YC), 16.0, 7.0, OP.mult, OP.add)
    ts(Li("sm"), Li("sm"), PF(1), None, OP.add)
    ts(LT(4, SC), Li("sm"), 1.0 / TH, 0.5 / TH - 0.5, OP.mult, OP.add)
    ts(LT(6, SC), LT(4, SC), float(-TH), None, OP.mult)
    tt(LT(6, SC), LT(6, SC), Li("sm"), OP.add)
    ts(LT(6, SC), LT(6, SC), 16.0, 15.0, OP.mult, OP.add)
    ts(LT(4, SC), LT(4, SC), -1.0, None, OP.add)
    tt(LT(4, SC), LT(4, SC), LT(4, SC), OP.mult)
    ts(LT(4, SC), LT(4, SC), 2.0, float(n), OP.min, OP.mult)
    tt(Li("sm"), LT(4, SC), LT(6, SC), OP.add)
    cp(L("sm"), Li("sm"))
    ts(PF(10), PF(5), 15.0, None, OP.add)
    ts(A("wb", 0, 144), A("xr", 0, 144), PF(10), 64.0, OP.is_equal, OP.mult)
    ts(PF(11), PF(0), 16.0, 15.0, OP.mult, OP.add)
    ts(A("wc", 0, 144), A("xr", 0, 144), PF(11), None, OP.is_equal)
    ts(A("wt", 0, 128), A("k16", 0, 128), PF(1), 416.0 / 2048, OP.is_equal, OP.mult)
    ts(A("dg", 0, 128), A("k16", 0, 128), PF(1), None, OP.is_equal)
    ts(A("i32", 0, 128), A("xr", 0, 128), PF(0), 32.0, OP.is_equal, OP.mult)
    act(A("in1", 0, 128), A("i32", 0, 128), AF.Identity, 0.0, -1.0 / 32)
    act(A("i20", 0, 128), A("i32", 0, 128), AF.Identity, 0.0, 32768.0)
    act(A("i21", 0, 128), A("i32", 0, 128), AF.Identity, 0.0, 65536.0)
    act(A("i22", 0, 128), A("i32", 0, 128), AF.Identity, 0.0, 131072.0)
    ms(A("one", 0, 128), 1.0)
    w2 = KQ * TH
    ms(A("cu", 0, 2 * n), -262144.0)
    for k0 in range(0, 16, REP):
        o = (k0 // KQ * 2 + 1) * w2 + k0 % KQ * TH
        ms(A("cu", o, o + REP * TH), -1024.0 if k0 >= 16 - VGT * REP else 0.0)
    ms(A("cb", 0, 16), -8388608.0)
    for jj in range(3):
        ms(A("cg", jj * n, (jj + 1) * n), 262144.0 * (1 - 16 * jj))
    act(A("ktf", 0, n), A("k16", 0, n), AF.Identity, 60.0 + me, -4.0)
    act(A("ktb", 0, n), A("k16", 0, n), AF.Identity, 60.0 + me, -4.0)
    ts(A("r16", 0, n), A("k16", 0, n), 0.0, None, OP.not_equal)
    ts(A("r4", 0, n), A("s4", 0, n), 0.0, None, OP.not_equal)
    ts(A("r4b", 0, n), A("s4", 0, n), 0.0, 4194304.0, OP.is_equal, OP.mult)
    cp(A("r4d", 0, n), A("r4", 0, n))
    ms(A("r4d", 3, n, 4), -1.0)
    cp(A("ldb", 0, 192, 1, 0, 8), A("ldi", 0, 192, 1, 0, 8))
    mm([(A("pm0", 0, 12), A("wc", 15 - r, 143 - r, 1, 0, 8), A("ldb", r, 192, 16, 0, 8), r == 0, r == 15) for r in range(16)])
    ms(A("ldl", 12, 16), 0.0)
    cp(A("ldl", 0, 12), A("pm0", 0, 12))
    ms(A("crd", 0, n), 0.0)
    ms(A("x3", 0, 16), float(4 * TH))
    for i in range(3):
        pos, seat = (3 * me + i) // NS, (3 * me + i) % NS
        for j, v in enumerate((2 - pos, pos - 1, pos)):
            ms(A("crd", 4 * i + j, n, 16), float(v))
            ms(A("x3", 4 * i + j, 4 * i + j + 1), float(j * RS + seat * SL + 4 * TH))
        ms(A("x3", 4 * i + 3, 4 * i + 4), float(i * RS + me * SL + 4 * TH))
    tt(A("x3", 16, 32), A("x3", 0, 16), A("dg", 0, 16), OP.mult)
    add("V", ("red", PF(12), A("x3", 16, 32)), [A("x3", 16, 32)], [PF(12)], 64)
    ts(L("RD"), Li("col"), PF(12), None, OP.add)
    one = A("one", 0, 128, 1, 0, 1)

    for h in range(NH):
        def B(name, lo, hi, step=1, p0=0, p1=128):
            o = h * ((_PER[name][0] + 15) // 16 * 16)
            return A(name, o + lo, o + hi, step, p0, p1)
        pm, pu = "pm%d" % h, "pu%d" % h
        tag[0] = h

        def m1(r, f0=0, f1=None, seat=me):
            o = M1R.index(r) * RS + seat * SL
            return B("m1", o + f0 * TH, o + (SL if f1 is None else f1 * TH))

        def m0(r, seat=me, w=SP):
            o = (r * NS + seat) * SP
            return B("m0", o, o + w)

        def m1w(r, k=1):
            return B("m1", M1R.index(r) * RS, (M1R.index(r) + k) * RS)

        def m2(r, seat=me):
            o = (M2R.index(r) * NS + seat) * n
            return B("m2", o, o + n)

        def m2w(r):
            return B("m2", M2R.index(r) * NS * n, (M2R.index(r) + 1) * NS * n)

        def send(kind, r):
            slot = {"a": m1, "y": m2, "p": m0}[kind]
            sem = "%s%d_%s" % (kind, h, r)
            far2 = kind == "y" or (r == "i" and h == 1)
            way = []
            for part, lat in (("far", XLAT), ("near", XLAT / 2)):
                s = add("G", ("send", kind, slot(r, seat=me), sem, part, far2), [slot(r, seat=me)], [], SEND / 2)
                way.append(add(None, ("way",), [], [], 0, lat - SEND / 2, None, [s]))
            add(None, ("arrive",), [], [slot(r, seat=q) for q in range(NS) if q != me], 0, 0, sem, way)

        def cc(d):
            return B("cc", d * n, (d + 1) * n)

        def ckp(d):
            return B("cp", d * n, (d + 1) * n)

        def ckl(d, lo=0, step=1):
            return B("ck", (2 * d + 1) * n + lo, (2 * d + 2) * n, step)

        def oh(j, lo=0, step=1):
            return B("oh", j * n + lo, (j + 1) * n, step)

        def se(j, lo=0, step=1, hi=n):
            return B("se", j * (n + 16) + lo, j * (n + 16) + hi, step)

        def no(jj):
            return B("no", jj * n, (jj + 1) * n)

        def suits(d):
            cp(B("ci", 0, n), ckl(d))
            ts(B("ci", n, 2 * n), B("ci", 0, n), 3, None, OP.bitwise_and)
            cp(B("ck", 2 * d * n, (2 * d + 1) * n), B("ci", n, 2 * n))

        def close(r, rec):
            tt(B("sm", 0, 16 * SC), IND(B("sc", 0, 3 * n), L("sm")), B("nl", 0, 16 * SC), OP.mult)
            ts(m1(r, 2, 5), B("sm", 0, 3 * TH), 0x7FFC3, None, OP.bitwise_and)
            if rec:
                ts(m1(r, 0, 1), B("sm", TH, 2 * TH), 6, 3, OP.arith_shift_right, OP.bitwise_and)
            send("a", r)
            if rec:
                ts(B("yu", 16 * YC, 16 * YC + TH), m1(r, 3, 4), 1.0 / 64, -32.0, OP.mult, OP.add)
                act(m2(r), IND(A("book", 0, 4096), B("yu", 16 * YC, 16 * YC + TH)), AF.Copy)
                send("y", r)

        def winner(j, r):
            tt(B("kk", 0, n), IND(B("m0", r * NS * SP, (r + 1) * NS * SP), L("K")), B("aa", 0, n), OP.add)
            scan(B("rw", 0, n), A("r4b", 0, n), B("kk", 0, n), OP.add, OP.min)
            tt(oh(j), IND(B("rw", 0, n), L("e3")), B("kk", 0, n), OP.is_equal)

        def pick(j, slot, r):
            tt(B("pr", 0, n), IND(m1w(r), L("P")), oh(j), OP.mult)
            scan(se(slot), A("r4", 0, n), B("pr", 0, n), OP.mult, OP.add)

        def redeal(d):
            w = [se(3 * d + 1 + i, 7, 16) for i in range(3)]

            def sa(i):
                return B("ss", 32 + 8 * i, 32 + 8 * i + TH)
            tt(sa(0), w[0], w[1], OP.is_le)
            tt(sa(1), w[0], w[2], OP.is_le)
            tt(sa(2), w[1], w[2], OP.is_le)
            tt(B("ss", 0, TH), sa(0), sa(1), OP.add)
            tt(B("ss", TH, 2 * TH), sa(0), sa(2), OP.subtract)
            tt(B("ss", 2 * TH, 3 * TH), sa(1), sa(2), OP.add)
            tt(B("kk", 0, n), IND(B("ss", 0, 4 * TH), L("SS")), A("crd", 0, n), OP.is_equal)
            tt(B("pr", 0, n), IND(m1w(3 * d, 3), L("RD")), B("kk", 0, n), OP.mult)
            scan(B("rw", 0, n), A("r4d", 0, n), B("pr", 0, n), OP.mult, OP.add)
            tt(B("x3", 0, 3 * n), IND(B("rw", 0, n), L("X3")), B("o3", 0, 3 * n), OP.mult)
            tt(B("x3", 3 * n, 4 * n), B("x3", 0, n), B("x3", n, 2 * n), OP.add)
            tt(B("x3", 4 * n, 5 * n), ckl(0) if d == 0 else B("cq", 0, n), B("x3", 2 * n, 3 * n), OP.subtract)
            tt(ckl(1) if d == 0 else B("x3", 0, n), B("x3", 4 * n, 5 * n), B("x3", 3 * n, 4 * n), OP.subtract)

        c0 = A("c0", h * n, (h + 1) * n)
        for r in M1R:
            iota(m1(r, 0, 2), [[0, 2], [16, TH]], me * n, 1)
            if SL > 5 * TH:
                ms(m1(r, 5), 0)
            if SP > TH and r in range(6):
                ms(m0(r), 0)
        ms(B("sc", 0, 3 * n), 0.0)
        ms(B("nl", 0, 16 * SC), 64.0)
        ms(B("nl", 0, TH), 2048.0)
        tt(ckp(0), c0, A("kc", 0, n), OP.add)
        ts(ckl(0), ckp(0), 32.0, None, OP.add)
        cp(B("sc", 15, n, 16), ckl(0, 0, 16))
        close("i", True)
        act(cc(0), c0, AF.Identity, -32.0, 1.0 / 64)
        suits(0)
        ms(B("ss", 3 * TH, 4 * TH), 0.0)
        ms(B("wn", 0, 16), 0.0)
        for j in range(8):
            ms(se(j, n, 1, n + 16), 0.0)
        ts(B("yu", 0, TH), L("col"), float(h * TH), None, OP.add)
        tt(oh(0), IND(A("ldl", 0, 16), B("yu", 0, TH)), A("s4", 0, n), OP.is_equal)

        for j in range(7):
            d, jj = j // 3, j % 3
            if j > 0:
                winner(j, j - 1)
            pick(j, j, "i" if j == 0 else j - 1)
            sl = j
            if j == 6:
                break
            if j == 3:
                redeal(0)
                scan(B("sc", 0, n), B("nr", 0, n), ckl(1), OP.mult, OP.max)
                close("b", True)
                act(ckp(1), ckl(1), AF.Identity, -32.0)
                tt(B("cq", 0, n), ckl(1), A("kc", 0, n), OP.subtract)
                act(cc(1), B("cq", 0, n), AF.Identity, -32.5, 1.0 / 64)
                suits(1)
                pick(j, 7, "b")
                sl = 7
            ry = "i" if j == 0 else "b" if j == 3 else j - 1
            mm([(A(pm, 0, TH), one, A("cb", 0, TH, 1, 0, 1), True, False)])
            mm([(A(pm, 0, TH), A("wt", 0, 128), se(j, 11, 16), False, False),
                (A(pm, 0, TH), A("i32", 0, 128), se(sl, 15, 16), False, True)])
            o = cc(d)[1]
            for th in range(TH):
                ts(B("zi", th, n, TH), A("cc", o + 16 * th, o + 16 * th + 16), se(sl, 16 * th + 15, 1, 16 * th + 16),
                   A(pm, th, th + 1), OP.mult, OP.add)
            ts(B("zi", n, 2 * n), B("zi", 0, n), 5, 4095, OP.arith_shift_right, OP.bitwise_and)
            cp(B("of", 0, n), B("zi", n, 2 * n))
            ts(B("yu", 0, 16 * YC), IND(se(sl), L("yl")), PF(5), None, OP.subtract)
            act(B("yr", 0, REP * n), IND(m2w(ry), B("yu", 0, REP * TH)), AF.Copy)
            act(B("aa", 0, n), oh(j), AF.Identity, 0.0, 261760.0)
            act(B("nl", 3 * TH, 4 * TH), oh(j, me, 16), AF.Identity, 1.0, -1.0)
            tt(se(sl, n, 1, n + TH), oh(j, me, 16), B("sc", 15, n, 16), OP.mult)
            tt(B("eq", 0, 2 * n), IND(se(sl, 0, 1, n + 16), A("lu", LOFF["e3"][0], LOFF["eq2"][1])),
               B("ck", 2 * d * n, (2 * d + 2) * n), OP.is_equal)
            pb = A(pm, 64, 64 + n)
            mm([(pb, one, A("ktb", 0, n, 1, 0, 1), True, False)]
               + [(pb, A("i22", 0, 128), no(i), False, False) for i in range(jj)])
            mm([(pb, A("i20", 0, 128), B("eq", 0, n), False, False), (pb, A("i21", 0, 128), B("eq", n, 2 * n), False, True)])
            act(B("bs", 0, n), pb, AF.Identity, 524288.0 - 4194304.0 * jj)
            pg = A(pm, 256, 256 + n)
            if j < 5:
                mm([(pg, one, A("ktb", 0, n, 1, 0, 1), True, False),
                    (pg, one, A("cg", jj * n, (jj + 1) * n, 1, 0, 1), False, False)]
                   + [(pg, A("i22", 0, 128), no(i), False, False) for i in range(jj)])
            for u in range(Q):
                ps = A(pu, 2 * w2 * u, 2 * w2 * (u + 1))
                mm([(ps, one, A("cu", 2 * w2 * u, 2 * w2 * (u + 1), 1, 0, 1), True, False)])
                for k0 in range(u * KQ, (u + 1) * KQ, REP):
                    dd = B("dd", k0 * n, (k0 + REP) * n)
                    tt(dd, IND(A("book", 0, 4096), B("of", k0 * TH, (k0 + REP) * TH)), B("yr", 0, REP * n), OP.subtract)
                    a0 = 2 * u * KQ * n + (k0 - u * KQ) * n
                    act(B("ab", a0, a0 + REP * n), dd, AF.Abs)
                    if k0 >= 16 - VGT * REP:
                        ts(B("ab", a0 + KQ * n, a0 + (KQ + REP) * n), dd, 0.0, 2.0, OP.is_gt, OP.mult)
                    else:
                        act(B("ab", a0 + KQ * n, a0 + (KQ + REP) * n), dd, AF.Sign, -0.5)
                mm([(ps, A("wb", 15 - r, 143 - r), B("ab", 2 * u * KQ * n + r, 2 * (u + 1) * KQ * n, 16),
                     False, r == 15) for r in range(16)])
            act(B("sg", 0, 3 * w2), A(pu, w2, 4 * w2), AF.Sign, 64.0, -1.0)
            tb = B("tb", 0, 3 * w2)
            tt(tb, B("sg", 0, 3 * w2), A(pu, 0, 3 * w2), OP.mult)
            ky, k2 = B("ky", 0, n), B("ky", n, 2 * n)
            tt(ky, IND(tb, L("perm")), B("bs", 0, n), OP.add)
            if j < 5:
                act(B("fp", 0, n), IND(tb, L("perm")), AF.Abs)
                mm([(pg, A("in1", 0, 128), B("fp", 0, n), False, True)])
            scan(B("sc", 2 * n, 3 * n), A("r16", 0, n), ky, OP.mult, OP.max)
            tt(B("sm", 32, 32 + TH), B("sc", 2 * n + 15, 3 * n, 16), B("nl", 3 * TH, 4 * TH), OP.mult)
            ts(m0(j, w=TH), B("sm", 32, 32 + TH), 0x7FFC3, None, OP.bitwise_and)
            send("p", j)
            tt(no(jj), IND(B("sc", 2 * n, 3 * n), L("e15")), ky, OP.not_equal)
            scan(B("sc", n, 2 * n), no(jj), ckp(d), OP.mult, OP.max)
            if jj == 2:
                close(j, False)
                act(B("o3", 0, 3 * n), B("no", 0, 3 * n), AF.Identity, 1.0 / 64, -1.0 / 64)
            if j < 5:
                tt(k2, no(jj), pg, OP.mult)
                if jj == 2:
                    tt(k2, k2, A("ktf", 0, n), OP.max)
                pv = A("pv", h * n, (h + 1) * n)
                scan(pv, A("r16", 0, n), k2, OP.mult, OP.max)
                tt(B("nr", 0, n), k2, pv, OP.not_equal)
                if jj < 2:
                    scan(B("sc", 0, n), B("nr", 0, n), ckl(d), OP.mult, OP.max)
                    close(j, True)
        redeal(1)
        turn(B("yo", 0, n), B("x3", 0, n), n, 2 * h * n, -32.0)
        add("Y", ("out", "yc", h, B("yo", 0, n)), [B("yo", 0, n)], [], 60, 2200, "dy%d" % h)
        mm([(A(pm, 0, TH), A("i32", 0, 128), oh(j, me, 16), j == 1, j == 6) for j in range(1, 7)])
        act(B("wn", 0, TH), A(pm, 0, TH), AF.Identity, 0.0, 1.0 / 32)
        tt(B("we", 0, n), IND(B("wn", 0, 16), L("col")), A("dg", 0, n), OP.mult)
        mm([(A(pm, 64, 64 + n, 1, 0, 8), A("wb", 15, 143, 16), B("we", 0, n), True, True)])
        act(B("wo", 0, n, 1, 0, 8), A(pm, 64, 64 + n, 1, 0, 8), AF.Identity, 0.0, 1.0 / 64)
        add("S", ("out", "yw", h, B("wo", 0, n, 1, 0, 8)), [B("wo", 0, n)], [], 60, 2200, "dw%d" % h)
    return ops


def deps(ops):
    hist, bank = {}, {}
    for i, o in enumerate(ops):
        dep = set(o["after"])
        for a in o["rd"]:
            m = cols(a)
            dep.update(j for j, w, mk in hist.get(a[0], ()) if w and mk & m)
        for a in o["wr"]:
            m = cols(a)
            dep.update(j for j, w, mk in hist.get(a[0], ()) if mk & m)
        for b in sorted(set(a[0] for a in o["rd"] + o["wr"] if psum(a) and a[0] != "pv")):
            e, cur, prev = bank.get(b, (None, [], []))
            if e == o["eng"]:
                dep.update(prev + (cur[-1:] if e == "P" else []))
                bank[b] = (e, cur + [i], prev)
            else:
                dep.update(cur)
                bank[b] = (o["eng"], [i], cur)
        for a in o["wr"]:
            m = cols(a)
            hist[a[0]] = [(j, w, mk & ~m) for j, w, mk in hist.get(a[0], ()) if mk & ~m] + [(i, True, m)]
        for a in o["rd"]:
            if a[0] != "book":
                hist.setdefault(a[0], []).append((i, False, cols(a)))
        dep.discard(i)
        o["dep"] = sorted(dep)
    return ops


PLAN = []


def plan():
    if PLAN:
        return PLAN[0]
    ops = deps(build(0))

    def gap(j, i):
        a, b = ops[j]["eng"], ops[i]["eng"]
        return 0 if a == b == "P" or b is None else W1 if a == b else W2
    N_ = len(ops)
    succ = [[] for _ in ops]
    for i, o in enumerate(ops):
        for j in o["dep"]:
            succ[j].append(i)
    pri = [0.0] * N_
    for i in range(N_ - 1, -1, -1):
        pri[i] = ops[i]["lat"] + max([pri[k] + gap(i, k) for k in succ[i]] + [0])
    pri = [p - STAG * o["h"] for p, o in zip(pri, ops)]
    left = [len(o["dep"]) for o in ops]
    rdy = [0.0] * N_
    free = {}
    pool = [i for i in range(N_) if not left[i]]
    order = []
    while pool:
        t0 = min(max(rdy[i], free.get(ops[i]["eng"], 0)) for i in pool)
        i = max((k for k in pool if max(rdy[k], free.get(ops[k]["eng"], 0)) <= t0 + TOL), key=lambda k: pri[k])
        pool.remove(i)
        o = ops[i]
        st = max(rdy[i], free.get(o["eng"], 0))
        if o["eng"]:
            free[o["eng"]] = st + o["busy"]
        o["t"] = st
        order.append(i)
        for k in succ[i]:
            fin = st + (o["busy"] if o["eng"] == ops[k]["eng"] == "P" else o["lat"])
            rdy[k] = max(rdy[k], fin + gap(i, k))
            left[k] -= 1
            if not left[k]:
                pool.append(k)
    PLAN.append((order, [o["t"] for o in ops]))
    return PLAN[0]


def messages(me):
    ops = build(me)
    return [ops[i]["what"] for i in plan()[0] if ops[i]["what"][0] == "send" and ops[i]["what"][4] == "far"]


def rank_program(g, core, T, topo):
    def ap(a):
        if not isinstance(a, tuple):
            return a
        if a[0] == "*":
            return ap(a[1]).indirect(ap(a[2]))
        return T[a[0]][a[4]:a[5], a[1]:a[2]:a[3]] if a[3] != 1 else T[a[0]][a[4]:a[5], a[1]:a[2]]

    me = T.rank_of(core)
    if me is None:
        for s, src in enumerate(T.cores):
            if core not in topo.cores_of(src):
                continue
            near, far, r1, r2 = routes(T, topo, src)
            if core not in r1 + r2:
                continue
            sent = 0
            for _, kind, slot, sem, part, far2 in messages(s):
                rl = r2 if far2 else r1
                if core in rl:
                    dst = far[rl.index(core)]
                    rid, pid = topo.addr(dst, core)
                    g.wait_ge(T.sem[sem], len(shares(T, topo, src)[rl.index(core)]))
                    g.remote_dma(ap(slot), ap(slot), T.sem[sem], T.sem.sent, pid, rid, topo.mask(core, dst))
                    sent += len(topo.engines(core, dst))
            g.wait_ge(T.sem.sent, sent)
        return

    near, far, r1, r2 = routes(T, topo, core)
    arrive = 0
    for src in T.cores:
        if src != core:
            arrive += len(topo.engines(src if src in near else routes(T, topo, src)[2][0], core))
    ops = deps(build(me))
    order, when = plan()
    queue = {"V": g.vector, "S": g.scalar, "P": g.tensor, "G": g, "Y": g.sync}
    count = {"V": 0, "S": 0, "P": 0, "G": 0}
    known = {e: {} for e in queue}
    sent = 0
    for i in order:
        o = ops[i]
        e, w = o["eng"], o["what"]
        if e is None:
            o["done"], o["clock"] = (o["sem"], arrive) if o["sem"] else None, {o["sem"]: arrive}
            continue
        q, kn = queue[e], known[e]
        need = {}
        for j in o["dep"]:
            p = ops[j]
            if p["done"] is None or e == p["eng"] == "P":
                continue
            if p["done"][1] > need.get(p["done"][0], (0, 0))[0]:
                need[p["done"][0]] = (p["done"][1], j)
        for s_, (v, j) in sorted(need.items(), key=lambda x: -when[x[1][1]]):
            if kn.get(s_, 0) < v:
                q.wait_ge(T.sem[s_], v)
                for s2, v2 in ops[j]["clock"].items():
                    kn[s2] = max(kn.get(s2, 0), v2)
        ins = []
        if w[0] == "tt":
            ins = [q.tensor_tensor(ap(w[1]), ap(w[2]), ap(w[3]), w[4])]
        elif w[0] == "ts":
            if w[6] is None:
                ins = [q.tensor_scalar(ap(w[1]), ap(w[2]), ap(w[3]), None, w[5])]
            else:
                ins = [q.tensor_scalar(ap(w[1]), ap(w[2]), ap(w[3]), ap(w[4]), w[5], w[6])]
        elif w[0] == "cp":
            ins = [q.tensor_copy(ap(w[1]), ap(w[2]))]
        elif w[0] == "scan":
            ins = [q.tensor_tensor_scan(ap(w[1]), ap(w[2]), ap(w[3]), 0.0, w[4], w[5])]
        elif w[0] == "ms":
            ins = [q.memset(ap(w[1]), w[2])]
        elif w[0] == "tr":
            ins = [q.transpose(ap(w[1]), ap(w[2]))]
        elif w[0] == "red":
            ins = [q.tensor_reduce(ap(w[1]), ap(w[2]), AxisListType.X, OP.add)]
        elif w[0] == "act":
            if w[3] == AF.Copy:
                ins = [q.activation(ap(w[1]), ap(w[2]), w[3])]
            else:
                ins = [q.activation(ap(w[1]), ap(w[2]), w[3], bias=w[4], scale=w[5])]
        elif w[0] == "mm":
            ins = [q.matmul(ap(a), ap(b), ap(c), s0, s1) for a, b, c, s0, s1 in w[1]]
        elif w[0] == "iota":
            if SCRATCH[w[1][0]][2] == I32:
                ins = [q.iota(ap(w[1]), w[2], w[3], w[4])]
            else:
                ins = [q.iota(ap(w[1]), w[2], w[3], w[4], allow_small_or_imprecise_dtypes=True)]
        elif w[0] == "dma":
            q.dma_start(ap(w[1]), T[w[2]][:]).then_inc(T.sem[o["sem"]], 16)
        elif w[0] == "out":
            q.dma_start(T[w[1]][:, w[2] * n:(w[2] + 1) * n], ap(w[3])).then_inc(T.sem[o["sem"]], 16)
        elif w[0] == "send":
            def transfer(c, es):
                rid, pid = topo.addr(c, core)
                return RemoteDMATransfer(dst_ids=[DstId(rid=rid, pnc=pid)], dma_engine_mask=bits(es),
                                         remote_sem=T.sem[w[3]], src=ap(w[2]), dst=ap(w[2]))
            if w[4] == "far":
                to = list(zip(r2 if w[5] else r1, shares(T, topo, core)))
            else:
                to = [(c, topo.engines(core, c)) for c in near]
            q.remote_dma_fused([transfer(c, es) for c, es in to], local_sem=T.sem.sent)
            sent += sum(len(es) for c, es in to)
        if w[0] == "send":
            o["done"] = None
        elif o["sem"]:
            o["done"] = (o["sem"], 16)
            o["clock"] = dict(kn)
            o["clock"][o["sem"]] = 16
        else:
            for x in ins:
                x.then_inc(T.sem[e], 1)
                count[e] += 1
            o["done"] = (e, count[e])
            o["clock"] = dict(kn)
            o["clock"][e] = count[e]
    for e in "VSPG":
        g.wait_ge(T.sem[e], count[e])
    g.wait_ge(T.sem.sent, sent)
    for h in range(NH):
        g.wait_ge(T.sem["dy%d" % h], 16)
        g.wait_ge(T.sem["dw%d" % h], 16)
